import numpy as np, ml_dtypes
CORES = [23,119,17,113]
N = 4
import mx_ref
BF = ml_dtypes.bfloat16
def pick(q, e):
    c = np.concatenate([q[0].reshape(128, -1, 4), np.zeros((128, 1, 4), np.uint8)], axis=1); s = np.concatenate([q[1], np.ones((16, 1), np.uint8)], axis=1)
    return (np.ascontiguousarray(c[:, e].reshape(128, -1)), np.ascontiguousarray(s[:, e]))
def join(*qs):
    return (np.concatenate([q[0] for q in qs], axis=1), np.concatenate([q[1] for q in qs], axis=1))
def put(q, e, v):
    c, s = q[0].reshape(128, -1, 4).copy(), q[1].copy(); c[:, e] = v[0].reshape(128, -1, 4); s[:, e] = v[1]
    return (c.reshape(128, -1), s)
def pk(c, s):
    return (np.ascontiguousarray(c), mx_ref.live(s))
def emit(q):
    return q[0], q[1]
def cut(t, i, w=512):
    return t[:, w * i:w * i + w]
def tile(rs):
    return np.stack(rs, axis=2).reshape(128, -1).astype(BF)
def f(rng, *shape):
    return mx_ref.flush((rng.standard_normal(shape, dtype=np.float32) * np.exp2(rng.integers(-2, 3, shape[:-1] + (1,)))).astype(BF))
def wide(rng, *shape, cols=0):
    v = rng.standard_normal(shape, dtype=np.float32) * np.exp2(rng.integers(-12, 13, shape)).astype(np.float32)
    if cols: v *= np.repeat(np.exp2(rng.integers(-cols, cols + 1, shape[:-2] + (1, shape[-1] // 4))) * (rng.random(shape[:-2] + (1, shape[-1] // 4)) > 0.0625), 4, axis=-1).astype(np.float32)
    return mx_ref.flush(v.astype(BF))
T, L, CAPP = 256, 2, 64
def game(x, u, w):
    S = [mx_ref.quantize(np.ascontiguousarray(x[r])) for r in range(N)]
    qu = [mx_ref.quantize(np.ascontiguousarray(u[r])) for r in range(N)]
    at, ks, made = np.arange(N * T).reshape(N, T), np.zeros((N, 1, L), np.float32), []
    for b in range(L):
        want = [np.flatnonzero(mx_ref.matmul(qu[r], S[r])[b] + np.float32(0) < 0) for r in range(N)]
        new, now = [], at.copy()
        for r in range(N):
            p = r ^ (1 << b)
            k = min(len(want[r]), len(want[p]), CAPP)
            to, of = want[r][:k], want[p][:k]
            c = pick(S[p], np.concatenate([of, np.full(CAPP - k, -1)]))
            t = tile([np.float32(0.0625) * mx_ref.matmul(mx_ref.quantize(np.ascontiguousarray(cut(w[r], 4 * b + i))), c) for i in range(4)])
            made.append(t)
            new.append(put(S[r], to, pick(mx_ref.quantize(t), np.arange(k))))
            now[r, to] = at[p, of]
            ks[r, 0, b] = k
        S, at = new, now
    return S, at, ks, made
def fit(t, low, high):
    a = np.abs(t.astype(np.float32))
    return bool((np.isfinite(a) & ((a == 0) | (a >= low) & (a <= high))).all())
def blocks(t):
    return np.abs(t.astype(np.float32)).reshape(16, 8, -1, 4).max(axis=(1, 3))
def plain(rng):
    u = np.array(f(rng, N, 128, 512))
    u[:, :, 4 * L:] = 0
    a = np.exp2(rng.integers(-2, 3, (N, 128, 1, 1)))
    x, lean = rng.standard_normal((N, 128, T, 4)), 2.5 * rng.random((N, L)) - 1
    for b in range(L):
        h = a * u[:, :, None, 4 * b:4 * b + 4].astype(np.float64)
        x += lean[:, b, None, None, None] * h * np.sum(h * h, axis=(1, 2, 3), keepdims=True) ** -0.5
    x = mx_ref.flush((a * x).reshape(N, 128, 4 * T).astype(np.float32).astype(BF))
    return {"x": x, "u": u, "w": f(rng, N, 128, 2048 * L), "v": f(rng, N, 128, 512)}
def aim(x, u, wish):
    x = x.reshape(N, 128, T, 4).astype(np.float32)
    for r in range(N):
        s = mx_ref.matmul(mx_ref.quantize(np.ascontiguousarray(u[r])), mx_ref.quantize(np.ascontiguousarray(x[r].reshape(128, 4 * T).astype(BF))))[0]
        x[r][:, s == 0] = u[r][:, None, :4].astype(np.float32)
        x[r][:, (s < 0) != wish[r]] *= -1
    return (x + np.float32(0)).reshape(N, 128, 4 * T).astype(BF)
def some(rng, n):
    return np.stack([rng.permutation(T) < n[r] for r in range(N)])
def setup_inputs(rng):
    return plain(rng)
def setup_inputs_many(rng):
    d = plain(rng)
    n = rng.integers(CAPP + 1, T + 1, N)
    j = 2 * int(rng.integers(0, N // 2))
    n[j:j + 2] = CAPP
    d["x"] = aim(d["x"], d["u"], some(rng, n))
    return d
def setup_inputs_none(rng):
    d = plain(rng)
    wish = some(rng, rng.integers(T // 4, T + 1, N))
    i, j = 2 * rng.permutation(N // 2)[:2] + rng.integers(0, 2, 2)
    wish[i] = False
    wish[i ^ 1] = True
    wish[j] = np.arange(T) == T - 1
    d["u"][int(rng.integers(0, N)), :, 4:8] = 0
    d["x"] = aim(d["x"], d["u"], wish)
    return d
def setup_inputs_zero(rng):
    d = plain(rng)
    d["u"][:, 64:, :4] = 0
    x = np.array(d["x"]).reshape(N, 128, T, 4)
    for r in range(N):
        e = rng.permutation(T)
        x[r][:, e[:T // 8]] = 0
        x[r][:64, e[T // 8:3 * T // 8]] = 0
    d["x"] = x.reshape(N, 128, 4 * T)
    return d
def setup_inputs_turn(rng):
    d = plain(rng)
    d["x"] = aim(d["x"], d["u"], some(rng, np.full(N, T // 2)))
    m, e = np.zeros((128, L, 4, 128, 4), np.float32), np.arange(128)
    for b in range(L):
        for i in range(4): m[e, b, i, e, i] = -16
    d["w"] = mx_ref.flush((m.reshape(128, 2048 * L) + d["w"].astype(np.float32) * np.float32(2.0 ** -6)).astype(BF))
    return d
def setup_inputs_spread(rng):
    d = plain(rng)
    u = np.array(wide(rng, N, 128, 512))
    u[:, :, 4 * L:] = 0
    return {**d, "x": wide(rng, N, 128, 4 * T, cols=6), "u": u, "v": wide(rng, N, 128, 512)}
def check_inputs(d):
    b = []
    for k in ("x", "u", "w", "v"):
        if not fit(d[k], 2.0 ** -30, 2.0 ** 30): b.append("a value of " + k)
    if (d["u"][:, :, 4 * L:].astype(np.float32) != 0).any(): b.append("u has numbers behind its first L columns")
    if not b:
        try:
            made = game(d["x"], d["u"], d["w"])[3]
            good, even = all(fit(t, 2.0 ** -60, 2.0 ** 60) for t in made), all(fit(blocks(t), 2.0 ** -30, 2.0 ** 30) for t in made)
        except Exception: good = even = False
        if not good: b.append("a number that an expert gives")
        if not even: b.append("the largest number of a block that an expert gives")
    return b
def reference(x, u, w, v):
    S, at, ks, made = game(x, u, w)
    oc, osc = np.zeros((N, 128, 4 * T), np.uint8), np.zeros((N, 16, T), np.uint8)
    y = np.zeros((N, 128, T), np.float32)
    for r in range(N):
        oc[r], osc[r] = emit(S[r])
        y[r] = mx_ref.matmul(mx_ref.quantize(np.ascontiguousarray(v[r])), S[r])
    return {"oc": oc, "osc": osc, "ids": at.reshape(N, 1, T).astype(np.float32), "ks": ks, "y": y}

@@ -1,0 +1,313 @@
+from concourse.bass import DstId, RemoteDMATransfer
+from concourse.mybir import dt, AluOpType as A, ActivationFunctionType as AF
+
+F8 = "float8_e4m3fn_x4"
+
+
+def _sb(n, t="float32"):
+    return ("sbuf", [128, n], t)
+
+
+SCRATCH = {
+    "ub": _sb(8, "bfloat16"), "xt": _sb(1024, "bfloat16"), "wt": _sb(4096, "bfloat16"), "vt": _sb(512, "bfloat16"),
+    "ut0": _sb(512, "bfloat16"), "ut1": _sb(512, "bfloat16"), "zt": _sb(512, "bfloat16"), "ones": _sb(256, "bfloat16"),
+    "h0": _sb(512, "bfloat16"), "h1": _sb(512, "bfloat16"),
+    "qu0c": _sb(128, F8), "qu0s": _sb(128, "uint8"), "qu1c": _sb(128, F8), "qu1s": _sb(128, "uint8"),
+    "qwc": _sb(1024, F8), "qws": _sb(1024, "uint8"), "qvc": _sb(128, F8), "qvs": _sb(128, "uint8"),
+    "hold0c": _sb(384, F8), "hold0s": _sb(384, "uint8"),
+    "hold1c": _sb(384, F8), "hold1s": _sb(384, "uint8"),
+    "finc": _sb(256, F8), "fins": _sb(256, "uint8"),
+    "snd0c": _sb(64, F8), "snd0s": _sb(64, "uint8"), "snd1c": _sb(64, F8), "snd1s": _sb(64, "uint8"),
+    "z0c": _sb(192, F8), "z0s": _sb(192, "uint8"), "z1c": _sb(192, F8), "z1s": _sb(192, "uint8"),
+    "w0": _sb(256, "bfloat16"), "w1": _sb(320, "bfloat16"), "wn": _sb(64, "bfloat16"),
+    "pidx": _sb(2, "int32"), "pand": _sb(2, "int32"), "pq": _sb(2), "r16": _sb(16), "rdup": _sb(32), "jw": _sb(16),
+    "offd": _sb(32, "uint16"), "bias": _sb(2), "thr": _sb(2), "alt": _sb(20), "c16": _sb(16),
+    "th": _sb(2), "ksb": _sb(2),
+    "cnt": _sb(1, "bfloat16"), "lin": _sb(4, "uint16"), "lin2": _sb(4, "uint16"), "pof": _sb(4, "uint16"),
+    "inf": _sb(8, "uint16"),
+    "tabp": _sb(256), "tabq": _sb(256), "pid": _sb(320), "ptmp": _sb(64),
+    "idw0": _sb(384), "idw1": _sb(384), "idf": _sb(256), "yrow": _sb(320), "yn": _sb(64),
+}
+for _b in range(2):
+    SCRATCH.update({
+        "d%d" % _b: _sb(256, "bfloat16"), "junk%d" % _b: _sb(512, "bfloat16"), "acc%d" % _b: _sb(2),
+        "mk%d" % _b: _sb(512, "bfloat16"), "scr%d" % _b: _sb(512, "bfloat16"), "off%d" % _b: _sb(8, "uint16"),
+        "dm%d" % _b: _sb(256, "bfloat16"), "dup%d" % _b: _sb(512, "bfloat16"), "dtr%d" % _b: _sb(512, "bfloat16"),
+        "lf%d" % _b: _sb(4), "idx%d" % _b: _sb(20), "gap%d" % _b: _sb(20), "sel%d" % _b: _sb(20), "mov%d" % _b: _sb(20),
+        "res%d" % _b: _sb(20), "offm%d" % _b: _sb(20, "uint16"),
+    })
+for _b in range(8):
+    SCRATCH["ps%d" % _b] = ("psum", [128, 512], "float32")
+
+REMOTE = ["rcnt", "rcod0", "rscl0", "rlst", "rpof", "rinf", "rcod1", "rscl1", "lcod0", "lall"]
+POOL = 80
+SEMAPHORES = REMOTE + ["s%d" % _i for _i in range(POOL)]
+
+
+def rank_program(g, core, T, topo):
+    rank = T.rank_of(core)
+    if rank is None:
+        return
+    cores = T.cores
+    mate0, mate1, far = rank ^ 1, rank ^ 2, rank ^ 3
+    V, S, P, Y = g.vector, g.scalar, g.tensor, g.sync
+    ops, local = [], {"lall": 0, "lcod0": 0}
+
+    def op(name, queue, fn, *deps, dma=False):
+        ops.append((name, queue, fn, deps, dma))
+
+    def eng(a, b):
+        return len(topo.engines(cores[a], cores[b]))
+    arrive = {"A.cnt": ("rcnt", eng(mate0, rank)), "A.cod0": ("rcod0", eng(mate0, rank)), "A.scl0": ("rscl0", eng(mate0, rank)),
+              "A.lst": ("rlst", eng(mate0, rank) + eng(far, rank)), "A.pof": ("rpof", eng(mate1, rank)),
+              "A.inf": ("rinf", eng(mate1, rank)), "A.cod1": ("rcod1", eng(mate1, rank)), "A.scl1": ("rscl1", eng(mate1, rank)),
+              "L.cod0": ("lcod0", eng(rank, mate0))}
+
+    def send(name, to, dst, src, sem, *deps, lsem="lall"):
+        rid, pid, _ = topo.addr(cores[to])
+        local[lsem] += eng(rank, to)
+        op(name, g, lambda: g.remote_dma(out_ap=dst, in_ap=src, remote_sem=T.sem[sem], local_sem=T.sem[lsem], pid=pid,
+                                         routing_id=rid, dma_engine_mask=topo.mask(core, cores[to])), *deps)
+
+    def u8(v):
+        return v.bitcast(dt.uint8)
+
+    def u32(v):
+        return v.bitcast(dt.uint32)
+
+    def mm(name, bank, n, wc, ws, xc, xs, *deps):
+        op(name, P, lambda: P.matmul_mx(T["ps%d" % bank][:, 0:n], wc, ws, xc, xs, True, True), *deps)
+
+    def ts(name, out, in0, s1, s2, o0, o1, *deps):
+        if o1 is None:
+            op(name, V, lambda: V.tensor_scalar(out, in0, s1, None, o0), *deps)
+        else:
+            op(name, V, lambda: V.tensor_scalar(out, in0, s1, s2, o0, o1), *deps)
+
+    def tt(name, out, a, b, o, *deps):
+        op(name, V, lambda: V.tensor_tensor(out, a, b, o), *deps)
+
+    def tc(name, out, in_, *deps):
+        op(name, V, lambda: V.tensor_copy(out, in_), *deps)
+
+    def scopy(name, out, in_, *deps, scale=None):
+        if scale is None:
+            op(name, S, lambda: S.activation(out, in_, AF.Copy), *deps)
+        else:
+            op(name, S, lambda: S.activation(out, in_, AF.Copy, scale=scale), *deps)
+
+    def quant(name, qc, qs, t, *deps):
+        op(name, V, lambda: V.quantize_mx(qc, qs, t), *deps)
+
+    def iota(name, out, pattern, base, cm, flag):
+        if flag:
+            op(name, g, lambda: g.iota(out, pattern, base, cm, allow_small_or_imprecise_dtypes=True))
+        else:
+            op(name, g, lambda: g.iota(out, pattern, base, cm))
+
+    op("ld.u", S, lambda: S.dma_start(T.ub[:, 0:8], T.u[:, 0:8]), dma=True)
+    op("ld.xA", Y, lambda: Y.dma_start(T.xt[:, 0:512], T.x[:, 0:512]), dma=True)
+    op("ld.xB", S, lambda: S.dma_start(T.xt[:, 512:1024], T.x[:, 512:1024]), dma=True)
+    op("ld.w0", Y, lambda: Y.dma_start(T.wt[:, 0:2048], T.w[:, 0:2048]), dma=True)
+
+    iota("i.p", T.pidx[:], [[0, 2]], 0, 1, False)
+    iota("i.r16", T.r16[:], [[16, 16]], 0, 0, True)
+    iota("i.dup", T.rdup[:], [[16, 16], [0, 2]], 0, 0, True)
+    iota("i.idw0", T.idw0[:], [[1, 384]], 256 * rank - 128, 0, True)
+    op("m.ones", V, lambda: V.memset(T.ones[:], 1.0))
+    op("m.zt", V, lambda: V.memset(T.zt[:], 0.0))
+    ts("c.and", T.pand[:], T.pidx[:], 15, None, A.bitwise_and, None, "i.p")
+    tc("c.pq", T.pq[:], T.pand[:], "c.and")
+    ts("c.jw", T.jw[:], T.r16[:], T.pq[:, 0:1], None, A.add, None, "c.pq", "i.r16")
+    ts("c.offd", T.offd[:], T.rdup[:], T.pq[:, 0:1], None, A.add, None, "c.pq", "i.dup")
+    ts("c.bias", T.bias[:], T.jw[:, 0:2], -255.5, None, A.add, None, "c.jw")
+    ts("c.thr", T.thr[:], T.jw[:, 2:4], -1.0, 256.0, A.mult, A.add, "c.jw")
+    for b in range(2):
+        ts("c.idx%d" % b, T["idx%d" % b][:, 0:4], T.jw[:, 0:4], -1.0, 255.0, A.mult, A.add, "c.jw")
+    ts("c.alt0", T.alt[:, 0:4], T.jw[:, 0:4], 256.0, None, A.add, None, "c.jw")
+    ts("c.alt1", T.alt[:, 4:20], T.jw[:], 128.0, None, A.add, None, "c.jw")
+    ts("c.c16", T.c16[:], T.jw[:], -1.0, 127.0, A.mult, A.add, "c.jw")
+    for b in range(2):
+        quant("q.z%d" % b, T["z%dc" % b][:, 64:192], T["z%ds" % b][:, 64:192], T.zt[:], "m.zt")
+        scopy("m.h%d" % b, T["h%d" % b][:, 256:512], T.zt[:, 0:256], "m.zt")
+
+    for t in (0, 1):
+        ts("u0.%d" % t, T.ut0[:, t:512:4], T.ones[:, 0:128], T.ub[:, t:t + 1], None, A.mult, None, "ld.u", "m.ones")
+
+    def fill(name, out, col):
+        op(name, S, lambda: S.activation(out, T.zt[:, 0:128], AF.Identity, bias=col), "ld.u", "m.zt")
+    for t in (2, 3):
+        fill("u0.%d" % t, T.ut0[:, t:512:4], T.ub[:, t:t + 1])
+    for t in range(4):
+        fill("u1.%d" % t, T.ut1[:, t:512:4], T.ub[:, 4 + t:5 + t])
+    quant("q.u0", T.qu0c[:], T.qu0s[:], T.ut0[:], "u0.0", "u0.1", "u0.2", "u0.3")
+
+    quant("q.xA", T.hold0c[:, 128:256], T.hold0s[:, 128:256], T.xt[:, 0:512], "ld.xA")
+    quant("q.xB", T.hold0c[:, 256:384], T.hold0s[:, 256:384], T.xt[:, 512:1024], "ld.xB")
+    mm("t.sA", 0, 128, T.qu0c[:], T.qu0s[:], T.hold0c[:, 128:256], T.hold0s[:, 128:256], "q.u0", "q.xA")
+    mm("t.sB", 1, 128, T.qu0c[:], T.qu0s[:], T.hold0c[:, 256:384], T.hold0s[:, 256:384], "q.u0", "q.xB")
+    ts("w.A", T.w0[:, 0:128], T.ps0[:, 0:128], 0.0, None, A.is_lt, None, "t.sA")
+    op("d.A", V, lambda: V.tensor_tensor_scan(T.d0[:, 0:128], T.ones[:, 0:128], T.w0[:, 0:128], 256.0, A.mult, A.subtract),
+       "w.A", "m.ones")
+    ts("w.B", T.w0[:, 128:256], T.ps1[:, 0:128], 0.0, None, A.is_lt, None, "t.sB")
+    op("d.0", V, lambda: V.tensor_tensor_scan(T.d0[:, 128:256], T.ones[:, 0:128], T.w0[:, 128:256], T.d0[:, 127:128],
+                                              A.mult, A.subtract), "w.B", "d.A")
+    send("g.cnt", mate0, T.cnt[:, 0:1], T.d0[:, 255:256], "rcnt", "d.0")
+
+    def lists(b):
+        d, acc, mk, scr, off, junk = (T[k % b] for k in ("d%d", "acc%d", "mk%d", "scr%d", "off%d", "junk%d"))
+        n = "d.%d" % b
+
+        def count_s(m):
+            op("ps%d.%d" % (m, b), S, lambda: S.activation(junk[:, 256 * m:256 * m + 255], d[:, 0:255], AF.Sign,
+                                                           bias=T.bias[:, m:m + 1], accum_out=acc[:, m:m + 1]), n, "c.bias")
+        count_s(0)
+        count_s(1)
+        ts("pm2.%d" % b, mk[:, 0:223], d[:, 32:255], T.thr[:, 0:1], None, A.is_ge, None, n, "c.thr")
+        ts("pm3.%d" % b, mk[:, 256:463], d[:, 48:255], T.thr[:, 1:2], None, A.is_ge, None, n)
+        op("pc2.%d" % b, V, lambda: V.tensor_tensor_scan(scr[:, 33:256], T.ones[:, 0:223], mk[:, 0:223], 32.0, A.mult, A.add),
+           "pm2.%d" % b)
+        op("pc3.%d" % b, V, lambda: V.tensor_tensor_scan(scr[:, 305:512], T.ones[:, 0:207], mk[:, 256:463], 48.0, A.mult, A.add),
+           "pm3.%d" % b)
+        if b:
+            tc("oc.1", off[:, 4:5], d[:, 255:256], n)
+        tc("ov.%d" % b, off[:, 2:4], scr[:, 255:512:256], "pc2.%d" % b, "pc3.%d" % b)
+        ts("os.%d" % b, off[:, 0:2], acc[:, 0:2], 0.5, 127.5, A.mult, A.add, "ps0.%d" % b, "ps1.%d" % b)
+
+    def pick(name, oc, os, ic, is_, off, deps):
+        op(name + "c", V, lambda: V.tensor_copy(u32(oc), u32(ic).indirect(off)), *deps)
+        op(name + "s", S, lambda: S.activation(os, is_.indirect(off), AF.Copy), *deps)
+
+    def wrap(b):
+        tt("dm.%d" % b, T["dm%d" % b][:], T["d%d" % b][:, 0:256], T["w%d" % b][:, 0:256], A.mult, "d.%d" % b)
+        scopy("dup.%d" % b, T["dup%d" % b][:], T["dm%d" % b][:, 0:256].indirect(T.offd[:, 0:32]), "dm.%d" % b, "c.offd")
+        if b == 0:
+            quant("q.u1", T.qu1c[:], T.qu1s[:], T.ut1[:], "u1.0", "u1.1", "u1.2", "u1.3")
+        tc("lf.%d" % b, T["lf%d" % b][:], T["off%d" % b][:, 0:4], "ov.%d" % b, "os.%d" % b)
+        tt("g4.%d" % b, T["gap%d" % b][:, 0:4], T["lf%d" % b][:], T.alt[:, 0:4], A.subtract, "lf.%d" % b, "c.alt0")
+        op("tr.%d" % b, V, lambda: V.transpose(T["dtr%d" % b][:], T["dup%d" % b][:]), "dup.%d" % b)
+        tc("ix.%d" % b, T["idx%d" % b][:, 4:20], T["dtr%d" % b][:, 0:512:32], "tr.%d" % b)
+        tt("g16.%d" % b, T["gap%d" % b][:, 4:20], T.c16[:], T["dtr%d" % b][:, 0:512:32], A.subtract, "tr.%d" % b, "c.c16")
+
+    def settle(b, cnt, ev):
+        ts("th.%d" % b, T.th[:, b:b + 1], cnt, T["d%d" % b][:, 255:256], 192.0, A.max, A.max, ev, "d.%d" % b)
+        ts("se.%d" % b, T["sel%d" % b][:], T["idx%d" % b][:], T.th[:, b:b + 1], None, A.is_ge, None,
+           "th.%d" % b, "ix.%d" % b, "c.idx%d" % b)
+        tt("mv.%d" % b, T["mov%d" % b][:], T["sel%d" % b][:], T["gap%d" % b][:], A.mult, "se.%d" % b, "g4.%d" % b, "g16.%d" % b)
+        tt("rs.%d" % b, T["res%d" % b][:], T["mov%d" % b][:], T.alt[:], A.add, "mv.%d" % b, "c.alt0", "c.alt1")
+        tc("om.%d" % b, T["offm%d" % b][:], T["res%d" % b][:], "rs.%d" % b)
+
+    def fresh(b):
+        z, h, hold = "z%d" % b, T["h%d" % b], "hold%d" % b
+        for i in range(4):
+            a = 512 * b + 128 * i
+            mm("R%d.%d" % (i, b), 4 + i, 128, T.qwc[:, a:a + 128], T.qws[:, a:a + 128], T[z + "c"][:, 0:128], T[z + "s"][:, 0:128],
+               "q.w%d" % b, "q.z%d" % b, "A.cod%d" % b, "A.scl%d" % b, *(("K%d.0" % i,) if b else ()))
+        for i in range(4):
+            if i % 2 == 0:
+                ts("K%d.%d" % (i, b), h[:, i:256:4], T["ps%d" % (4 + i)][:, 0:64], 0.0625, None, A.mult, None, "R%d.%d" % (i, b))
+            else:
+                scopy("K%d.%d" % (i, b), h[:, i:256:4], T["ps%d" % (4 + i)][:, 0:64], "R%d.%d" % (i, b), scale=0.0625)
+        quant("q.n%d" % b, T[hold + "c"][:, 0:128], T[hold + "s"][:, 0:128], h[:],
+              *["K%d.%d" % (i, b) for i in range(4)], "m.h%d" % b)
+
+    lists(0)
+    pick("pk0", T.snd0c[:], T.snd0s[:], T.hold0c[:, 128:384], T.hold0s[:, 128:384], T.off0[:, 0:4], ("ov.0", "os.0", "q.xA", "q.xB"))
+    send("g.cod0", mate0, u8(T.z0c[:, 0:64]), u8(T.snd0c[:, 0:64]), "rcod0", "pk0c", lsem="lcod0")
+    send("g.scl0", mate0, T.z0s[:, 0:64], T.snd0s[:, 0:64], "rscl0", "pk0s")
+    to = [topo.addr(cores[r]) for r in (mate0, far)]
+    local["lall"] += eng(rank, mate0)
+    op("g.lst", g, lambda: g.remote_dma_fused([RemoteDMATransfer(
+        dst_ids=[DstId(rid=a[0], pnc=a[1]) for a in to],
+        dma_engine_mask=topo.mask(core, cores[mate0]) & topo.mask(core, cores[far]),
+        remote_sem=T.sem["rlst"], srcs=[T.off0[:, 0:4]], dsts=[T.lin[:], T.lin2[:]])], local_sem=T.sem["lall"]), "ov.0", "os.0")
+    op("ld.w1", Y, lambda: Y.dma_start(T.wt[:, 2048:4096], T.w[:, 2048:4096]), "L.cod0", dma=True)
+    op("ld.v", Y, lambda: Y.dma_start(T.vt[:], T.v[:]), dma=True)
+    iota("i.tabp", T.tabp[:], [[1, 256]], 256 * mate0, 0, True)
+    iota("i.tabq", T.tabq[:], [[1, 256]], 256 * far, 0, True)
+    iota("i.pid", T.pid[:], [[1, 320]], 256 * mate1, 0, True)
+    iota("i.idw1", T.idw1[:, 64:128], [[1, 64]], 0, 0, True)
+
+    wrap(0)
+    mm("t.s1", 2, 256, T.qu1c[:], T.qu1s[:], T.hold0c[:, 128:384], T.hold0s[:, 128:384], "q.u1", "q.xA", "q.xB")
+    quant("q.w0", T.qwc[:, 0:512], T.qws[:, 0:512], T.wt[:, 0:2048], "ld.w0")
+    ts("w.1x", T.w1[:, 0:256], T.ps2[:, 0:256], 0.0, None, A.is_lt, None, "t.s1")
+    settle(0, T.cnt[:, 0:1], "A.cnt")
+    send("g.pof", mate1, T.pof[:], T.offm0[:, 0:4], "rpof", "om.0")
+
+    fresh(0)
+    mm("t.sN", 0, 128, T.qu1c[:], T.qu1s[:], T.hold0c[:, 0:128], T.hold0s[:, 0:128], "q.n0", "w.A")
+    pick("mg0", T.hold1c[:, 128:384], T.hold1s[:, 128:384], T.hold0c[:, 0:384], T.hold0s[:, 0:384], T.offm0[:, 4:20],
+         ("om.0", "q.n0", "q.xA", "q.xB"))
+    scopy("id.a", T.idw0[:, 0:64], T.tabp[:].indirect(T.lin[:, 0:4]), "A.lst", "i.tabp", "i.idw0")
+    scopy("id.p", T.ptmp[:], T.tabq[:].indirect(T.lin2[:, 0:4]), "A.lst", "i.tabq")
+    ts("w.N", T.wn[:], T.ps0[:, 0:64], 0.0, None, A.is_lt, None, "t.sN")
+    tc("w.1", T.w1[:, 0:320].indirect(T.offm0[:, 0:4]), T.wn[:], "w.N", "w.1x", "om.0")
+    op("d.1", V, lambda: V.tensor_tensor_scan(T.d1[:], T.ones[:], T.w1[:, 0:256], 256.0, A.mult, A.subtract), "w.1")
+
+    lists(1)
+    send("g.inf", mate1, T.inf[:, 0:5], T.off1[:, 0:5], "rinf", "oc.1", "ov.1", "os.1")
+    pick("pk1", T.snd1c[:], T.snd1s[:], T.hold1c[:, 128:384], T.hold1s[:, 128:384], T.off1[:, 0:4], ("ov.1", "os.1", "mg0c", "mg0s"))
+    send("g.cod1", mate1, u8(T.z1c[:, 0:64]), u8(T.snd1c[:, 0:64]), "rcod1", "pk1c")
+    send("g.scl1", mate1, T.z1s[:, 0:64], T.snd1s[:, 0:64], "rscl1", "pk1s")
+    wrap(1)
+    quant("q.w1", T.qwc[:, 512:1024], T.qws[:, 512:1024], T.wt[:, 2048:4096], "ld.w1")
+    quant("q.v", T.qvc[:], T.qvs[:], T.vt[:], "ld.v")
+    mm("t.y", 3, 256, T.qvc[:], T.qvs[:], T.hold1c[:, 128:384], T.hold1s[:, 128:384], "q.v", "mg0c", "mg0s")
+    tc("id.q", T.pid[:, 0:320].indirect(T.pof[:, 0:4]), T.ptmp[:], "A.pof", "id.p", "i.pid")
+    scopy("id.m", T.idw1[:, 128:384], T.idw0[:].indirect(T.offm0[:, 4:20]), "id.a", "i.idw0", "om.0")
+    scopy("y.m", T.yrow[:, 0:256], T.ps3[:, 0:256], "t.y")
+    settle(1, T.inf[:, 4:5], "A.inf")
+    ts("ks", T.ksb[:], T.th[:], -1.0, 256.0, A.mult, A.add, "th.0", "th.1")
+    scopy("id.n", T.idw1[:, 0:64], T.pid[:, 0:256].indirect(T.inf[:, 0:4]), "id.q", "A.inf")
+    fresh(1)
+    scopy("id.f", T.idf[:], T.idw1[:].indirect(T.offm1[:, 4:20]), "id.m", "id.n", "i.idw1", "om.1")
+    mm("t.yn", 1, 128, T.qvc[:], T.qvs[:], T.hold1c[:, 0:128], T.hold1s[:, 0:128], "q.n1", "q.v", "w.B")
+    scopy("y.n", T.yn[:], T.ps1[:, 0:64], "t.yn")
+    pick("mg1", T.finc[:], T.fins[:], T.hold1c[:, 0:384], T.hold1s[:, 0:384], T.offm1[:, 4:20], ("om.1", "q.n1", "mg0c", "mg0s"))
+    tc("y.s", T.yrow[:, 0:320].indirect(T.offm1[:, 0:4]), T.yn[:], "y.n", "y.m", "om.1")
+
+    op("st.k", Y, lambda: Y.dma_start(T.ks[0:1, 0:2], T.ksb[0:1, 0:2]), "ks", dma=True)
+    op("st.i", Y, lambda: Y.dma_start(T.ids[0:1, :], T.idf[0:1, :]), "id.f", dma=True)
+    op("st.c", Y, lambda: Y.dma_start(T.oc[:, :], u8(T.finc[:, 0:256])), "mg1c", dma=True)
+    op("st.y", Y, lambda: Y.dma_start(T.y[:, :], T.yrow[:, 0:256]), "y.s", dma=True)
+
+    def scales(q, k):
+        op("st.s%d" % k, q, lambda: q.dma_start(T.osc[4 * k:4 * k + 4, 0:256], T.fins[32 * k:32 * k + 4, 0:256]), "mg1s", dma=True)
+    for k in range(4):
+        scales(S if k < 2 else Y, k)
+    op("end", Y, None, "st.k", "st.i", "st.c", "st.y", "st.s0", "st.s1", "st.s2", "st.s3")
+
+    qs = (g, V, S, P, Y)
+    known, seen, waits, needed = [set() for _ in qs], {}, [], set()
+
+    def number(q):
+        return [i for i in range(5) if qs[i] is q][0]
+    for name, q, fn, deps, dma in ops:
+        i, w = number(q), []
+        for dep in deps:
+            if dep not in known[i]:
+                w.append(dep)
+                known[i] |= {dep} | seen.get(dep, set())
+                needed.add(dep)
+        seen[name] = set(known[i])
+        waits.append(w)
+    pool, mark = [], {e: arrive[e] for e in arrive}
+    for name, q, fn, deps, dma in ops:
+        if name in needed:
+            i = number(q)
+            old = [s for s in pool if not dma and s[0] == i and s[2] in seen[name]]
+            if old:
+                old[0][2], old[0][3] = name, old[0][3] + 1
+                mark[name] = (old[0][1], old[0][3])
+            else:
+                pool.append([-1 if dma else i, "s%d" % len(pool), name, 16 if dma else 1])
+                mark[name] = (pool[-1][1], pool[-1][3])
+    for (name, q, fn, deps, dma), w in zip(ops, waits):
+        for dep in w:
+            q.wait_ge(T.sem[mark[dep][0]], mark[dep][1])
+        if fn is not None:
+            ins = fn()
+            if name in needed:
+                ins.then_inc(T.sem[mark[name][0]], 16 if dma else 1)
+    g.wait_ge(T.sem["lall"], local["lall"])

@@ -1,7 +1,7 @@
 from concourse.bass import DstId, RemoteDMATransfer
 from concourse.mybir import dt, AluOpType as A, ActivationFunctionType as AF
 
-F8 = "float8_e4m3fn_x4"
+F8, BF = "float8_e4m3fn_x4", "bfloat16"
 
 
 def _sb(n, t="float32"):
@@ -9,37 +9,26 @@ def _sb(n, t="float32"):
 
 
 SCRATCH = {
-    "ub": _sb(8, "bfloat16"), "xt": _sb(1024, "bfloat16"), "wt": _sb(4096, "bfloat16"), "vt": _sb(512, "bfloat16"),
-    "ut0": _sb(512, "bfloat16"), "ut1": _sb(512, "bfloat16"), "zt": _sb(512, "bfloat16"), "ones": _sb(256, "bfloat16"),
-    "h0": _sb(512, "bfloat16"), "h1": _sb(512, "bfloat16"),
-    "qu0c": _sb(128, F8), "qu0s": _sb(128, "uint8"), "qu1c": _sb(128, F8), "qu1s": _sb(128, "uint8"),
-    "qwc": _sb(1024, F8), "qws": _sb(1024, "uint8"), "qvc": _sb(128, F8), "qvs": _sb(128, "uint8"),
-    "hold0c": _sb(384, F8), "hold0s": _sb(384, "uint8"),
-    "hold1c": _sb(384, F8), "hold1s": _sb(384, "uint8"),
-    "finc": _sb(256, F8), "fins": _sb(256, "uint8"),
-    "snd0c": _sb(64, F8), "snd0s": _sb(64, "uint8"), "snd1c": _sb(64, F8), "snd1s": _sb(64, "uint8"),
-    "z0c": _sb(192, F8), "z0s": _sb(192, "uint8"), "z1c": _sb(192, F8), "z1s": _sb(192, "uint8"),
-    "w0": _sb(256, "bfloat16"), "w1": _sb(320, "bfloat16"), "wn": _sb(64, "bfloat16"),
-    "pidx": _sb(2, "int32"), "pand": _sb(2, "int32"), "pq": _sb(2), "r16": _sb(16), "rdup": _sb(32), "jw": _sb(16),
-    "offd": _sb(32, "uint16"), "bias": _sb(2), "thr": _sb(2), "alt": _sb(20), "c16": _sb(16),
-    "th": _sb(2), "ksb": _sb(2),
-    "cnt": _sb(1, "bfloat16"), "lin": _sb(4, "uint16"), "lin2": _sb(4, "uint16"), "pof": _sb(4, "uint16"),
-    "inf": _sb(8, "uint16"),
-    "tabp": _sb(256), "tabq": _sb(256), "pid": _sb(320), "ptmp": _sb(64),
-    "idw0": _sb(384), "idw1": _sb(384), "idf": _sb(256), "yrow": _sb(320), "yn": _sb(64),
+    "cnt0": _sb(1, BF), "cnt1": _sb(1, BF), "lin": _sb(4, "uint16"), "lin2": _sb(4, "uint16"), "pof": _sb(4, "uint16"),
+    "lin1": _sb(4, "uint16"), "offd": _sb(32, "uint16"), "pidx": _sb(2, "int32"), "pand": _sb(2, "int32"), "pand2": _sb(2, "int32"),
 }
-for _b in range(2):
-    SCRATCH.update({
-        "d%d" % _b: _sb(256, "bfloat16"), "junk%d" % _b: _sb(512, "bfloat16"), "acc%d" % _b: _sb(2),
-        "mk%d" % _b: _sb(512, "bfloat16"), "scr%d" % _b: _sb(512, "bfloat16"), "off%d" % _b: _sb(8, "uint16"),
-        "dm%d" % _b: _sb(256, "bfloat16"), "dup%d" % _b: _sb(512, "bfloat16"), "dtr%d" % _b: _sb(512, "bfloat16"),
-        "lf%d" % _b: _sb(4), "idx%d" % _b: _sb(20), "gap%d" % _b: _sb(20), "sel%d" % _b: _sb(20), "mov%d" % _b: _sb(20),
-        "res%d" % _b: _sb(20), "offm%d" % _b: _sb(20, "uint16"),
-    })
+for _n, _k in dict(ub=8, xt=1024, wt=4096, vt=512, ut0=512, ut1=512, zt=512, ones=256, h0=512, h1=512, w0=256, w1=320, wn=64).items():
+    SCRATCH[_n] = _sb(_k, BF)
+for _n, _k in dict(qu0=128, qu1=128, qw=1024, qv=128, hold0=384, hold1=384, fin=256, snd0=64, snd1=64, z0=192, z1=192).items():
+    SCRATCH[_n + "c"], SCRATCH[_n + "s"] = _sb(_k, F8), _sb(_k, "uint8")
+for _n, _k in dict(pq=2, hq=2, hs=2, r16=16, rdup=32, jw=16, bias=2, thr=2, alt=20, c16=16, th=2, ksb=2, tabp=256, tabq=256, pid=320,
+                   ptmp=64, idw0=384, idw1=384, idf=256, yrow=320, yn=64).items():
+    SCRATCH[_n] = _sb(_k)
+for _b in "01":
+    for _n, _k in dict(d=272, junk=512, mk=512, scr=512, dup=512, dtr=512).items():
+        SCRATCH[_n + _b] = _sb(_k, BF)
+    for _n, _k in dict(acc=2, wl=16, lf=4, idx=20, gap=20, sel=20, mov=20, res=20).items():
+        SCRATCH[_n + _b] = _sb(_k)
+    SCRATCH["off" + _b], SCRATCH["offm" + _b] = _sb(4, "uint16"), _sb(20, "uint16")
 for _b in range(8):
     SCRATCH["ps%d" % _b] = ("psum", [128, 512], "float32")
 
-REMOTE = ["rcnt", "rcod0", "rscl0", "rlst", "rpof", "rinf", "rcod1", "rscl1", "lcod0", "lall"]
+REMOTE = ["rcnt0", "rcod0", "rscl0", "rlst", "rpof", "rcnt1", "rlst1", "rcod1", "rscl1", "lall", "lcnt0", "go"]
 POOL = 80
 SEMAPHORES = REMOTE + ["s%d" % _i for _i in range(POOL)]
 
@@ -51,17 +40,18 @@ def rank_program(g, core, T, topo):
     cores = T.cores
     mate0, mate1, far = rank ^ 1, rank ^ 2, rank ^ 3
     V, S, P, Y = g.vector, g.scalar, g.tensor, g.sync
-    ops, local = [], {"lall": 0, "lcod0": 0}
+    ops, local = [], {"lall": 0, "lcnt0": 0}
 
     def op(name, queue, fn, *deps, dma=False):
         ops.append((name, queue, fn, deps, dma))
 
     def eng(a, b):
         return len(topo.engines(cores[a], cores[b]))
-    arrive = {"A.cnt": ("rcnt", eng(mate0, rank)), "A.cod0": ("rcod0", eng(mate0, rank)), "A.scl0": ("rscl0", eng(mate0, rank)),
-              "A.lst": ("rlst", eng(mate0, rank) + eng(far, rank)), "A.pof": ("rpof", eng(mate1, rank)),
-              "A.inf": ("rinf", eng(mate1, rank)), "A.cod1": ("rcod1", eng(mate1, rank)), "A.scl1": ("rscl1", eng(mate1, rank)),
-              "L.cod0": ("lcod0", eng(rank, mate0))}
+    arrive = {"A.lst": ("rlst", eng(mate0, rank) + eng(far, rank)), "A.pof": ("rpof", eng(mate1, rank)),
+              "A.lst1": ("rlst1", eng(mate1, rank)), "E.go": ("go", 1), "L.cnt0": ("lcnt0", eng(rank, mate0))}
+    for b, m in ((0, mate0), (1, mate1)):
+        for kind in ("cnt", "cod", "scl"):
+            arrive["A.%s%d" % (kind, b)] = ("r%s%d" % (kind, b), eng(m, rank))
 
     def send(name, to, dst, src, sem, *deps, lsem="lall"):
         rid, pid, _ = topo.addr(cores[to])
@@ -90,6 +80,9 @@ def rank_program(g, core, T, topo):
     def tc(name, out, in_, *deps):
         op(name, V, lambda: V.tensor_copy(out, in_), *deps)
 
+    def scan(name, out, a, b, init, o, *deps):
+        op(name, V, lambda: V.tensor_tensor_scan(out, a, b, init, A.mult, o), *deps)
+
     def scopy(name, out, in_, *deps, scale=None):
         if scale is None:
             op(name, S, lambda: S.activation(out, in_, AF.Copy), *deps)
@@ -99,16 +92,19 @@ def rank_program(g, core, T, topo):
     def quant(name, qc, qs, t, *deps):
         op(name, V, lambda: V.quantize_mx(qc, qs, t), *deps)
 
+    def move(name, q, out, in_, *deps):
+        op(name, q, lambda: q.dma_start(out, in_), *deps, dma=True)
+
     def iota(name, out, pattern, base, cm, flag):
         if flag:
             op(name, g, lambda: g.iota(out, pattern, base, cm, allow_small_or_imprecise_dtypes=True))
         else:
             op(name, g, lambda: g.iota(out, pattern, base, cm))
 
-    op("ld.u", S, lambda: S.dma_start(T.ub[:, 0:8], T.u[:, 0:8]), dma=True)
-    op("ld.xA", Y, lambda: Y.dma_start(T.xt[:, 0:512], T.x[:, 0:512]), dma=True)
-    op("ld.xB", S, lambda: S.dma_start(T.xt[:, 512:1024], T.x[:, 512:1024]), dma=True)
-    op("ld.w0", Y, lambda: Y.dma_start(T.wt[:, 0:2048], T.w[:, 0:2048]), dma=True)
+    move("ld.u", S, T.ub[:, 0:8], T.u[:, 0:8])
+    move("ld.xA", Y, T.xt[:, 0:512], T.x[:, 0:512])
+    move("ld.xB", Y, T.xt[:, 512:1024], T.x[:, 512:1024])
+    move("ld.w0", Y, T.wt[:, 0:2048], T.w[:, 0:2048])
 
     iota("i.p", T.pidx[:], [[0, 2]], 0, 1, False)
     iota("i.r16", T.r16[:], [[16, 16]], 0, 0, True)
@@ -117,60 +113,54 @@ def rank_program(g, core, T, topo):
     op("m.ones", V, lambda: V.memset(T.ones[:], 1.0))
     op("m.zt", V, lambda: V.memset(T.zt[:], 0.0))
     ts("c.and", T.pand[:], T.pidx[:], 15, None, A.bitwise_and, None, "i.p")
+    ts("c.and2", T.pand2[:], T.pidx[:], 16, None, A.bitwise_and, None, "i.p")
     tc("c.pq", T.pq[:], T.pand[:], "c.and")
+    tc("c.hq", T.hq[:], T.pand2[:], "c.and2")
     ts("c.jw", T.jw[:], T.r16[:], T.pq[:, 0:1], None, A.add, None, "c.pq", "i.r16")
-    ts("c.offd", T.offd[:], T.rdup[:], T.pq[:, 0:1], None, A.add, None, "c.pq", "i.dup")
+    ts("c.hs", T.hs[:], T.hq[:], -0.0625, 16.0, A.mult, A.add, "c.hq")
+
+    def front(b):
+        op("m.d%d" % b, V, lambda t=T["d%d" % b]: V.memset(t[:, 0:16], 256.0))
+
+    def rest(b):
+        ts("c.idx%d" % b, T["idx%d" % b][:, 0:4], T.jw[:, 0:4], -1.0, 255.0, A.mult, A.add, "c.jw")
+        quant("q.z%d" % b, T["z%dc" % b][:, 64:192], T["z%ds" % b][:, 64:192], T.zt[:], "m.zt")
+    front(0)
+    ts("c.offd", T.offd[:], T.rdup[:], T.pq[:, 0:1], T.hs[:, 0:1], A.add, A.add, "c.pq", "c.hs", "i.dup")
     ts("c.bias", T.bias[:], T.jw[:, 0:2], -255.5, None, A.add, None, "c.jw")
     ts("c.thr", T.thr[:], T.jw[:, 2:4], -1.0, 256.0, A.mult, A.add, "c.jw")
     for b in range(2):
-        ts("c.idx%d" % b, T["idx%d" % b][:, 0:4], T.jw[:, 0:4], -1.0, 255.0, A.mult, A.add, "c.jw")
-    ts("c.alt0", T.alt[:, 0:4], T.jw[:, 0:4], 256.0, None, A.add, None, "c.jw")
-    ts("c.alt1", T.alt[:, 4:20], T.jw[:], 128.0, None, A.add, None, "c.jw")
-    ts("c.c16", T.c16[:], T.jw[:], -1.0, 127.0, A.mult, A.add, "c.jw")
-    for b in range(2):
-        quant("q.z%d" % b, T["z%dc" % b][:, 64:192], T["z%ds" % b][:, 64:192], T.zt[:], "m.zt")
         scopy("m.h%d" % b, T["h%d" % b][:, 256:512], T.zt[:, 0:256], "m.zt")
 
-    for t in (0, 1):
+    for t in range(4):
         ts("u0.%d" % t, T.ut0[:, t:512:4], T.ones[:, 0:128], T.ub[:, t:t + 1], None, A.mult, None, "ld.u", "m.ones")
 
     def fill(name, out, col):
         op(name, S, lambda: S.activation(out, T.zt[:, 0:128], AF.Identity, bias=col), "ld.u", "m.zt")
-    for t in (2, 3):
-        fill("u0.%d" % t, T.ut0[:, t:512:4], T.ub[:, t:t + 1])
     for t in range(4):
         fill("u1.%d" % t, T.ut1[:, t:512:4], T.ub[:, 4 + t:5 + t])
     quant("q.u0", T.qu0c[:], T.qu0s[:], T.ut0[:], "u0.0", "u0.1", "u0.2", "u0.3")
 
+    X = ("q.xA", "q.xB")
     quant("q.xA", T.hold0c[:, 128:256], T.hold0s[:, 128:256], T.xt[:, 0:512], "ld.xA")
     quant("q.xB", T.hold0c[:, 256:384], T.hold0s[:, 256:384], T.xt[:, 512:1024], "ld.xB")
     mm("t.sA", 0, 128, T.qu0c[:], T.qu0s[:], T.hold0c[:, 128:256], T.hold0s[:, 128:256], "q.u0", "q.xA")
     mm("t.sB", 1, 128, T.qu0c[:], T.qu0s[:], T.hold0c[:, 256:384], T.hold0s[:, 256:384], "q.u0", "q.xB")
     ts("w.A", T.w0[:, 0:128], T.ps0[:, 0:128], 0.0, None, A.is_lt, None, "t.sA")
-    op("d.A", V, lambda: V.tensor_tensor_scan(T.d0[:, 0:128], T.ones[:, 0:128], T.w0[:, 0:128], 256.0, A.mult, A.subtract),
-       "w.A", "m.ones")
+    scan("d.A", T.d0[:, 16:144], T.ones[:, 0:128], T.w0[:, 0:128], 256.0, A.subtract, "w.A", "m.ones")
     ts("w.B", T.w0[:, 128:256], T.ps1[:, 0:128], 0.0, None, A.is_lt, None, "t.sB")
-    op("d.0", V, lambda: V.tensor_tensor_scan(T.d0[:, 128:256], T.ones[:, 0:128], T.w0[:, 128:256], T.d0[:, 127:128],
-                                              A.mult, A.subtract), "w.B", "d.A")
-    send("g.cnt", mate0, T.cnt[:, 0:1], T.d0[:, 255:256], "rcnt", "d.0")
+    scan("d.0", T.d0[:, 144:272], T.ones[:, 0:128], T.w0[:, 128:256], T.d0[:, 143:144], A.subtract, "w.B", "d.A")
 
     def lists(b):
         d, acc, mk, scr, off, junk = (T[k % b] for k in ("d%d", "acc%d", "mk%d", "scr%d", "off%d", "junk%d"))
         n = "d.%d" % b
-
-        def count_s(m):
-            op("ps%d.%d" % (m, b), S, lambda: S.activation(junk[:, 256 * m:256 * m + 255], d[:, 0:255], AF.Sign,
-                                                           bias=T.bias[:, m:m + 1], accum_out=acc[:, m:m + 1]), n, "c.bias")
-        count_s(0)
-        count_s(1)
-        ts("pm2.%d" % b, mk[:, 0:223], d[:, 32:255], T.thr[:, 0:1], None, A.is_ge, None, n, "c.thr")
-        ts("pm3.%d" % b, mk[:, 256:463], d[:, 48:255], T.thr[:, 1:2], None, A.is_ge, None, n)
-        op("pc2.%d" % b, V, lambda: V.tensor_tensor_scan(scr[:, 33:256], T.ones[:, 0:223], mk[:, 0:223], 32.0, A.mult, A.add),
-           "pm2.%d" % b)
-        op("pc3.%d" % b, V, lambda: V.tensor_tensor_scan(scr[:, 305:512], T.ones[:, 0:207], mk[:, 256:463], 48.0, A.mult, A.add),
-           "pm3.%d" % b)
-        if b:
-            tc("oc.1", off[:, 4:5], d[:, 255:256], n)
+        for m in range(2):
+            op("ps%d.%d" % (m, b), S, lambda m=m: S.activation(junk[:, 256 * m:256 * m + 255], d[:, 16:271], AF.Sign,
+                                                               bias=T.bias[:, m:m + 1], accum_out=acc[:, m:m + 1]), n, "c.bias")
+        ts("pm2.%d" % b, mk[:, 0:223], d[:, 48:271], T.thr[:, 0:1], None, A.is_ge, None, n, "c.thr")
+        ts("pm3.%d" % b, mk[:, 256:463], d[:, 64:271], T.thr[:, 1:2], None, A.is_ge, None, n)
+        scan("pc2.%d" % b, scr[:, 33:256], T.ones[:, 0:223], mk[:, 0:223], 32.0, A.add, "pm2.%d" % b)
+        scan("pc3.%d" % b, scr[:, 305:512], T.ones[:, 0:207], mk[:, 256:463], 48.0, A.add, "pm3.%d" % b)
         tc("ov.%d" % b, off[:, 2:4], scr[:, 255:512:256], "pc2.%d" % b, "pc3.%d" % b)
         ts("os.%d" % b, off[:, 0:2], acc[:, 0:2], 0.5, 127.5, A.mult, A.add, "ps0.%d" % b, "ps1.%d" % b)
 
@@ -178,42 +168,58 @@ def rank_program(g, core, T, topo):
         op(name + "c", V, lambda: V.tensor_copy(u32(oc), u32(ic).indirect(off)), *deps)
         op(name + "s", S, lambda: S.activation(os, is_.indirect(off), AF.Copy), *deps)
 
+    def merge(b, i, p, q, *deps):
+        oc, os, c = (T.finc, T.fins, 0) if b else (T.hold1c, T.hold1s, 128)
+        pick("mg%d%d" % (b, i), oc[:, c + p:c + q], os[:, c + p:c + q], T["hold%dc" % b][:, 0:384], T["hold%ds" % b][:, 0:384],
+             T["offm%d" % b][:, 4 + p // 16:4 + q // 16], ("om.%d" % b, "q.n%d" % b) + deps)
+
     def wrap(b):
-        tt("dm.%d" % b, T["dm%d" % b][:], T["d%d" % b][:, 0:256], T["w%d" % b][:, 0:256], A.mult, "d.%d" % b)
-        scopy("dup.%d" % b, T["dup%d" % b][:], T["dm%d" % b][:, 0:256].indirect(T.offd[:, 0:32]), "dm.%d" % b, "c.offd")
-        if b == 0:
-            quant("q.u1", T.qu1c[:], T.qu1s[:], T.ut1[:], "u1.0", "u1.1", "u1.2", "u1.3")
+        dp, dq = T["dtr%d" % b][:, 0:512:32], T["dtr%d" % b][:, 16:512:32]
+        scopy("dup.%d" % b, T["dup%d" % b][:], T["d%d" % b][:, 0:272].indirect(T.offd[:, 0:32]), "d.%d" % b, "c.offd", "m.d%d" % b)
         tc("lf.%d" % b, T["lf%d" % b][:], T["off%d" % b][:, 0:4], "ov.%d" % b, "os.%d" % b)
         tt("g4.%d" % b, T["gap%d" % b][:, 0:4], T["lf%d" % b][:], T.alt[:, 0:4], A.subtract, "lf.%d" % b, "c.alt0")
+        if b == 0:
+            ts("w.1x", T.w1[:, 0:256], T.ps2[:, 0:256], 0.0, None, A.is_lt, None, "t.s1")
         op("tr.%d" % b, V, lambda: V.transpose(T["dtr%d" % b][:], T["dup%d" % b][:]), "dup.%d" % b)
-        tc("ix.%d" % b, T["idx%d" % b][:, 4:20], T["dtr%d" % b][:, 0:512:32], "tr.%d" % b)
-        tt("g16.%d" % b, T["gap%d" % b][:, 4:20], T.c16[:], T["dtr%d" % b][:, 0:512:32], A.subtract, "tr.%d" % b, "c.c16")
+        tt("wl.%d" % b, T["wl%d" % b][:], dp, dq, A.is_lt, "tr.%d" % b)
+        tt("g16.%d" % b, T["gap%d" % b][:, 4:20], T.c16[:], dp, A.subtract, "tr.%d" % b, "c.c16")
+        tt("ix.%d" % b, T["idx%d" % b][:, 4:20], T["wl%d" % b][:], dp, A.mult, "wl.%d" % b)
 
-    def settle(b, cnt, ev):
-        ts("th.%d" % b, T.th[:, b:b + 1], cnt, T["d%d" % b][:, 255:256], 192.0, A.max, A.max, ev, "d.%d" % b)
-        ts("se.%d" % b, T["sel%d" % b][:], T["idx%d" % b][:], T.th[:, b:b + 1], None, A.is_ge, None,
-           "th.%d" % b, "ix.%d" % b, "c.idx%d" % b)
-        tt("mv.%d" % b, T["mov%d" % b][:], T["sel%d" % b][:], T["gap%d" % b][:], A.mult, "se.%d" % b, "g4.%d" % b, "g16.%d" % b)
-        tt("rs.%d" % b, T["res%d" % b][:], T["mov%d" % b][:], T.alt[:], A.add, "mv.%d" % b, "c.alt0", "c.alt1")
-        tc("om.%d" % b, T["offm%d" % b][:], T["res%d" % b][:], "rs.%d" % b)
+    def settle(b, part):
+        if part == 0:
+            ts("th.%d" % b, T.th[:, b:b + 1], T["cnt%d" % b][:, 0:1], T["d%d" % b][:, 271:272], 192.0, A.max, A.max,
+               "A.cnt%d" % b, "d.%d" % b)
+        if part == 1:
+            ts("se.%d" % b, T["sel%d" % b][:], T["idx%d" % b][:], T.th[:, b:b + 1], None, A.is_ge, None,
+               "th.%d" % b, "ix.%d" % b, "c.idx%d" % b)
+        if part == 2:
+            tt("mv.%d" % b, T["mov%d" % b][:], T["sel%d" % b][:], T["gap%d" % b][:], A.mult, "se.%d" % b, "g4.%d" % b, "g16.%d" % b)
+        if part == 3:
+            tt("rs.%d" % b, T["res%d" % b][:], T["mov%d" % b][:], T.alt[:], A.add, "mv.%d" % b, "c.alt0", "c.alt1")
+            tc("om.%d" % b, T["offm%d" % b][:], T["res%d" % b][:], "rs.%d" % b)
+
+    def expert(b, i):
+        a, c = 512 * b + 128 * i, 2048 * b + 512 * i
+        quant("q.w%d%d" % (i, b), T.qwc[:, a:a + 128], T.qws[:, a:a + 128], T.wt[:, c:c + 512], "ld.w%d" % b)
 
     def fresh(b):
         z, h, hold = "z%d" % b, T["h%d" % b], "hold%d" % b
         for i in range(4):
             a = 512 * b + 128 * i
             mm("R%d.%d" % (i, b), 4 + i, 128, T.qwc[:, a:a + 128], T.qws[:, a:a + 128], T[z + "c"][:, 0:128], T[z + "s"][:, 0:128],
-               "q.w%d" % b, "q.z%d" % b, "A.cod%d" % b, "A.scl%d" % b, *(("K%d.0" % i,) if b else ()))
+               "q.w%d%d" % (i, b), "q.z%d" % b, "A.cod%d" % b, "A.scl%d" % b, *(("K%d.0" % i,) if b else ()))
         for i in range(4):
-            if i % 2 == 0:
+            if i == 3:
                 ts("K%d.%d" % (i, b), h[:, i:256:4], T["ps%d" % (4 + i)][:, 0:64], 0.0625, None, A.mult, None, "R%d.%d" % (i, b))
             else:
                 scopy("K%d.%d" % (i, b), h[:, i:256:4], T["ps%d" % (4 + i)][:, 0:64], "R%d.%d" % (i, b), scale=0.0625)
         quant("q.n%d" % b, T[hold + "c"][:, 0:128], T[hold + "s"][:, 0:128], h[:],
               *["K%d.%d" % (i, b) for i in range(4)], "m.h%d" % b)
 
+    send("g.cnt0", mate0, T.cnt0[:, 0:1], T.d0[:, 271:272], "rcnt0", "d.0", lsem="lcnt0")
     lists(0)
-    pick("pk0", T.snd0c[:], T.snd0s[:], T.hold0c[:, 128:384], T.hold0s[:, 128:384], T.off0[:, 0:4], ("ov.0", "os.0", "q.xA", "q.xB"))
-    send("g.cod0", mate0, u8(T.z0c[:, 0:64]), u8(T.snd0c[:, 0:64]), "rcod0", "pk0c", lsem="lcod0")
+    pick("pk0", T.snd0c[:], T.snd0s[:], T.hold0c[:, 128:384], T.hold0s[:, 128:384], T.off0[:, 0:4], ("ov.0", "os.0") + X)
+    send("g.cod0", mate0, u8(T.z0c[:, 0:64]), u8(T.snd0c[:, 0:64]), "rcod0", "pk0c")
     send("g.scl0", mate0, T.z0s[:, 0:64], T.snd0s[:, 0:64], "rscl0", "pk0s")
     to = [topo.addr(cores[r]) for r in (mate0, far)]
     local["lall"] += eng(rank, mate0)
@@ -221,61 +227,75 @@ def rank_program(g, core, T, topo):
         dst_ids=[DstId(rid=a[0], pnc=a[1]) for a in to],
         dma_engine_mask=topo.mask(core, cores[mate0]) & topo.mask(core, cores[far]),
         remote_sem=T.sem["rlst"], srcs=[T.off0[:, 0:4]], dsts=[T.lin[:], T.lin2[:]])], local_sem=T.sem["lall"]), "ov.0", "os.0")
-    op("ld.w1", Y, lambda: Y.dma_start(T.wt[:, 2048:4096], T.w[:, 2048:4096]), "L.cod0", dma=True)
-    op("ld.v", Y, lambda: Y.dma_start(T.vt[:], T.v[:]), dma=True)
+    op("g.go", g, lambda: g.sem_inc(T.sem["go"], 1))
+    move("ld.v", Y, T.vt[:], T.v[:], "E.go", "L.cnt0")
+    move("ld.w1", Y, T.wt[:, 2048:4096], T.w[:, 2048:4096])
     iota("i.tabp", T.tabp[:], [[1, 256]], 256 * mate0, 0, True)
     iota("i.tabq", T.tabq[:], [[1, 256]], 256 * far, 0, True)
     iota("i.pid", T.pid[:], [[1, 320]], 256 * mate1, 0, True)
     iota("i.idw1", T.idw1[:, 64:128], [[1, 64]], 0, 0, True)
 
+    quant("q.u1", T.qu1c[:], T.qu1s[:], T.ut1[:], "u1.0", "u1.1", "u1.2", "u1.3")
+    mm("t.s1", 2, 256, T.qu1c[:], T.qu1s[:], T.hold0c[:, 128:384], T.hold0s[:, 128:384], "q.u1", *X)
+    ts("c.alt0", T.alt[:, 0:4], T.jw[:, 0:4], 256.0, None, A.add, None, "c.jw")
+    ts("c.alt1", T.alt[:, 4:20], T.jw[:], 128.0, None, A.add, None, "c.jw")
+    ts("c.c16", T.c16[:], T.jw[:], -1.0, 127.0, A.mult, A.add, "c.jw")
+    rest(0)
     wrap(0)
-    mm("t.s1", 2, 256, T.qu1c[:], T.qu1s[:], T.hold0c[:, 128:384], T.hold0s[:, 128:384], "q.u1", "q.xA", "q.xB")
-    quant("q.w0", T.qwc[:, 0:512], T.qws[:, 0:512], T.wt[:, 0:2048], "ld.w0")
-    ts("w.1x", T.w1[:, 0:256], T.ps2[:, 0:256], 0.0, None, A.is_lt, None, "t.s1")
-    settle(0, T.cnt[:, 0:1], "A.cnt")
+    for i, part in ((0, None), (1, 0), (2, 1), (3, 2)):
+        expert(0, i)
+        if part is not None:
+            settle(0, part)
+    settle(0, 3)
+    front(1)
+    rest(1)
     send("g.pof", mate1, T.pof[:], T.offm0[:, 0:4], "rpof", "om.0")
 
     fresh(0)
     mm("t.sN", 0, 128, T.qu1c[:], T.qu1s[:], T.hold0c[:, 0:128], T.hold0s[:, 0:128], "q.n0", "w.A")
-    pick("mg0", T.hold1c[:, 128:384], T.hold1s[:, 128:384], T.hold0c[:, 0:384], T.hold0s[:, 0:384], T.offm0[:, 4:20],
-         ("om.0", "q.n0", "q.xA", "q.xB"))
-    scopy("id.a", T.idw0[:, 0:64], T.tabp[:].indirect(T.lin[:, 0:4]), "A.lst", "i.tabp", "i.idw0")
-    scopy("id.p", T.ptmp[:], T.tabq[:].indirect(T.lin2[:, 0:4]), "A.lst", "i.tabq")
+    merge(0, 0, 0, 160, *X)
     ts("w.N", T.wn[:], T.ps0[:, 0:64], 0.0, None, A.is_lt, None, "t.sN")
+    merge(0, 1, 160, 192, *X)
     tc("w.1", T.w1[:, 0:320].indirect(T.offm0[:, 0:4]), T.wn[:], "w.N", "w.1x", "om.0")
-    op("d.1", V, lambda: V.tensor_tensor_scan(T.d1[:], T.ones[:], T.w1[:, 0:256], 256.0, A.mult, A.subtract), "w.1")
+    merge(0, 2, 192, 224, *X)
+    scan("d.1", T.d1[:, 16:272], T.ones[:], T.w1[:, 0:256], 256.0, A.subtract, "w.1")
 
+    send("g.cnt1", mate1, T.cnt1[:, 0:1], T.d1[:, 271:272], "rcnt1", "d.1")
+    merge(0, 3, 224, 256, *X)
     lists(1)
-    send("g.inf", mate1, T.inf[:, 0:5], T.off1[:, 0:5], "rinf", "oc.1", "ov.1", "os.1")
-    pick("pk1", T.snd1c[:], T.snd1s[:], T.hold1c[:, 128:384], T.hold1s[:, 128:384], T.off1[:, 0:4], ("ov.1", "os.1", "mg0c", "mg0s"))
+    M = tuple("mg0%d%s" % (i, k) for i in range(4) for k in "cs")
+    pick("pk1", T.snd1c[:], T.snd1s[:], T.hold1c[:, 128:384], T.hold1s[:, 128:384], T.off1[:, 0:4], ("ov.1", "os.1") + M)
     send("g.cod1", mate1, u8(T.z1c[:, 0:64]), u8(T.snd1c[:, 0:64]), "rcod1", "pk1c")
     send("g.scl1", mate1, T.z1s[:, 0:64], T.snd1s[:, 0:64], "rscl1", "pk1s")
-    wrap(1)
-    quant("q.w1", T.qwc[:, 512:1024], T.qws[:, 512:1024], T.wt[:, 2048:4096], "ld.w1")
+    send("g.lst1", mate1, T.lin1[:], T.off1[:, 0:4], "rlst1", "ov.1", "os.1")
     quant("q.v", T.qvc[:], T.qvs[:], T.vt[:], "ld.v")
-    mm("t.y", 3, 256, T.qvc[:], T.qvs[:], T.hold1c[:, 128:384], T.hold1s[:, 128:384], "q.v", "mg0c", "mg0s")
+    mm("t.y", 3, 256, T.qvc[:], T.qvs[:], T.hold1c[:, 128:384], T.hold1s[:, 128:384], "q.v", *M)
+    for i in range(4):
+        expert(1, i)
+    settle(1, 0)
+    wrap(1)
+    scopy("id.p", T.ptmp[:], T.tabq[:].indirect(T.lin2[:, 0:4]), "A.lst", "i.tabq")
+    scopy("id.a", T.idw0[:, 0:64], T.tabp[:].indirect(T.lin[:, 0:4]), "A.lst", "i.tabp", "i.idw0")
     tc("id.q", T.pid[:, 0:320].indirect(T.pof[:, 0:4]), T.ptmp[:], "A.pof", "id.p", "i.pid")
+    for part in (1, 2, 3):
+        settle(1, part)
+    ts("ks", T.ksb[:], T.th[:], -1.0, 256.0, A.mult, A.add, "th.0", "th.1")
     scopy("id.m", T.idw1[:, 128:384], T.idw0[:].indirect(T.offm0[:, 4:20]), "id.a", "i.idw0", "om.0")
     scopy("y.m", T.yrow[:, 0:256], T.ps3[:, 0:256], "t.y")
-    settle(1, T.inf[:, 4:5], "A.inf")
-    ts("ks", T.ksb[:], T.th[:], -1.0, 256.0, A.mult, A.add, "th.0", "th.1")
-    scopy("id.n", T.idw1[:, 0:64], T.pid[:, 0:256].indirect(T.inf[:, 0:4]), "id.q", "A.inf")
     fresh(1)
+    scopy("id.n", T.idw1[:, 0:64], T.pid[:, 0:256].indirect(T.lin1[:, 0:4]), "id.q", "A.lst1")
     scopy("id.f", T.idf[:], T.idw1[:].indirect(T.offm1[:, 4:20]), "id.m", "id.n", "i.idw1", "om.1")
     mm("t.yn", 1, 128, T.qvc[:], T.qvs[:], T.hold1c[:, 0:128], T.hold1s[:, 0:128], "q.n1", "q.v", "w.B")
     scopy("y.n", T.yn[:], T.ps1[:, 0:64], "t.yn")
-    pick("mg1", T.finc[:], T.fins[:], T.hold1c[:, 0:384], T.hold1s[:, 0:384], T.offm1[:, 4:20], ("om.1", "q.n1", "mg0c", "mg0s"))
+    merge(1, 0, 0, 256, *M)
     tc("y.s", T.yrow[:, 0:320].indirect(T.offm1[:, 0:4]), T.yn[:], "y.n", "y.m", "om.1")
 
-    op("st.k", Y, lambda: Y.dma_start(T.ks[0:1, 0:2], T.ksb[0:1, 0:2]), "ks", dma=True)
-    op("st.i", Y, lambda: Y.dma_start(T.ids[0:1, :], T.idf[0:1, :]), "id.f", dma=True)
-    op("st.c", Y, lambda: Y.dma_start(T.oc[:, :], u8(T.finc[:, 0:256])), "mg1c", dma=True)
-    op("st.y", Y, lambda: Y.dma_start(T.y[:, :], T.yrow[:, 0:256]), "y.s", dma=True)
-
-    def scales(q, k):
-        op("st.s%d" % k, q, lambda: q.dma_start(T.osc[4 * k:4 * k + 4, 0:256], T.fins[32 * k:32 * k + 4, 0:256]), "mg1s", dma=True)
+    move("st.k", Y, T.ks[0:1, 0:2], T.ksb[0:1, 0:2], "ks")
+    move("st.c", Y, T.oc[:, :], u8(T.finc[:, 0:256]), "mg10c")
+    move("st.y", Y, T.y[:, :], T.yrow[:, 0:256], "y.s")
     for k in range(4):
-        scales(S if k < 2 else Y, k)
+        move("st.s%d" % k, S if k < 2 else Y, T.osc[4 * k:4 * k + 4, 0:256], T.fins[32 * k:32 * k + 4, 0:256], "mg10s")
+    move("st.i", S, T.ids[0:1, :], T.idf[0:1, :], "id.f")
     op("end", Y, None, "st.k", "st.i", "st.c", "st.y", "st.s0", "st.s1", "st.s2", "st.s3")
 
     qs = (g, V, S, P, Y)

@@ -9,28 +9,32 @@ def _sb(n, t="float32"):
 
 
 SCRATCH = {
-    "cnt0": _sb(1, BF), "cnt1": _sb(1, BF), "lin": _sb(4, "uint16"), "lin2": _sb(4, "uint16"), "pof": _sb(4, "uint16"),
-    "lin1": _sb(4, "uint16"), "offd": _sb(32, "uint16"), "pidx": _sb(2, "int32"), "pand": _sb(2, "int32"), "pand2": _sb(2, "int32"),
+    "cna": _sb(1), "cnb": _sb(1, BF), "cnta": _sb(1), "cntb": _sb(1, BF), "cnt1": _sb(1, BF),
+    "lin": _sb(4, "uint16"), "lin2": _sb(4, "uint16"), "pof": _sb(4, "uint16"),
+    "lin1": _sb(4, "uint16"), "offd": _sb(16, "uint16"), "pidx": _sb(2, "int32"), "pand": _sb(2, "int32"), "pand2": _sb(2, "int32"),
 }
-for _n, _k in dict(ub=8, xt=1024, wt=4096, vt=512, ut0=512, ut1=512, zt=512, ones=256, h0=512, h1=512, w0=256, w1=320, wn=64).items():
+for _n, _k in dict(ub=8, xt=1024, wt=4096, vt=512, ut0=512, ut1=512, zt=512, ones=128, h0=512, h1=512, w0=288, w1=352, wn=64,
+                   sig=256, siga=128).items():
     SCRATCH[_n] = _sb(_k, BF)
-for _n, _k in dict(qu0=128, qu1=128, qw=1024, qv=128, hold0=384, hold1=384, fin=256, snd0=64, snd1=64, z0=192, z1=192).items():
+for _n, _k in dict(qu0=128, qu1=128, qw=1024, qv=128, hold0=384, hold1=384, fin=256, snd0=64, snd1=64, z=256).items():
     SCRATCH[_n + "c"], SCRATCH[_n + "s"] = _sb(_k, F8), _sb(_k, "uint8")
-for _n, _k in dict(pq=2, hq=2, hs=2, r16=16, rdup=32, jw=16, bias=2, thr=2, alt=20, c16=16, th=2, ksb=2, tabp=256, tabq=256, pid=320,
-                   ptmp=64, idw0=384, idw1=384, idf=256, yrow=320, yn=64).items():
+for _n, _k in dict(pq=2, p31=2, r16=16, r32=16, jw=16, bias=2, lo=2, hi=2, ini=2, alt=20, acnt=1, th=2, ksb=2, row=256, pid=336,
+                   ptmp=64, idw0=384, idw1=384, idf=256, yrow=336, yn=64).items():
     SCRATCH[_n] = _sb(_k)
 for _b in "01":
-    for _n, _k in dict(d=272, junk=512, mk=512, scr=512, dup=512, dtr=512).items():
+    for _n, _k in dict(f=272, junk=256, clip=256, sums=256, wb=256, e=256, dup=256, dtr=256).items():
         SCRATCH[_n + _b] = _sb(_k, BF)
-    for _n, _k in dict(acc=2, wl=16, lf=4, idx=20, gap=20, sel=20, mov=20, res=20).items():
+    for _n, _k in dict(acc=2, lf=4, gap=20, sel=20, mov=20, res=20).items():
         SCRATCH[_n + _b] = _sb(_k)
     SCRATCH["off" + _b], SCRATCH["offm" + _b] = _sb(4, "uint16"), _sb(20, "uint16")
 for _b in range(8):
     SCRATCH["ps%d" % _b] = ("psum", [128, 512], "float32")
 
-REMOTE = ["rcnt0", "rcod0", "rscl0", "rlst", "rpof", "rcnt1", "rlst1", "rcod1", "rscl1", "lall", "lcnt0", "go"]
+REMOTE = ["rcnta", "rcntb", "rcod0", "rscl0", "rlst", "rpof", "rcnt1", "rlst1", "rcod1", "rscl1", "lall", "lcnt", "go"]
 POOL = 80
 SEMAPHORES = REMOTE + ["s%d" % _i for _i in range(POOL)]
+Z = (0, 128)
+NEW = (0, 64)
 
 
 def rank_program(g, core, T, topo):
@@ -40,7 +44,7 @@ def rank_program(g, core, T, topo):
     cores = T.cores
     mate0, mate1, far = rank ^ 1, rank ^ 2, rank ^ 3
     V, S, P, Y = g.vector, g.scalar, g.tensor, g.sync
-    ops, local = [], {"lall": 0, "lcnt0": 0}
+    ops, local = [], {"lall": 0, "lcnt": 0}
 
     def op(name, queue, fn, *deps, dma=False):
         ops.append((name, queue, fn, deps, dma))
@@ -48,9 +52,11 @@ def rank_program(g, core, T, topo):
     def eng(a, b):
         return len(topo.engines(cores[a], cores[b]))
     arrive = {"A.lst": ("rlst", eng(mate0, rank) + eng(far, rank)), "A.pof": ("rpof", eng(mate1, rank)),
-              "A.lst1": ("rlst1", eng(mate1, rank)), "E.go": ("go", 1), "L.cnt0": ("lcnt0", eng(rank, mate0))}
+              "A.lst1": ("rlst1", eng(mate1, rank)), "A.cnt1": ("rcnt1", eng(mate1, rank)),
+              "A.cnta": ("rcnta", eng(mate0, rank)), "A.cntb": ("rcntb", eng(mate0, rank)),
+              "E.go": ("go", 1), "L.cnt": ("lcnt", eng(rank, mate0))}
     for b, m in ((0, mate0), (1, mate1)):
-        for kind in ("cnt", "cod", "scl"):
+        for kind in ("cod", "scl"):
             arrive["A.%s%d" % (kind, b)] = ("r%s%d" % (kind, b), eng(m, rank))
 
     def send(name, to, dst, src, sem, *deps, lsem="lall"):
@@ -80,14 +86,11 @@ def rank_program(g, core, T, topo):
     def tc(name, out, in_, *deps):
         op(name, V, lambda: V.tensor_copy(out, in_), *deps)
 
-    def scan(name, out, a, b, init, o, *deps):
-        op(name, V, lambda: V.tensor_tensor_scan(out, a, b, init, A.mult, o), *deps)
+    def scan(name, out, a, b, init, o0, o1, *deps):
+        op(name, V, lambda: V.tensor_tensor_scan(out, a, b, init, o0, o1), *deps)
 
-    def scopy(name, out, in_, *deps, scale=None):
-        if scale is None:
-            op(name, S, lambda: S.activation(out, in_, AF.Copy), *deps)
-        else:
-            op(name, S, lambda: S.activation(out, in_, AF.Copy, scale=scale), *deps)
+    def act(name, out, in_, fn, *deps, **kw):
+        op(name, S, lambda: S.activation(out, in_, fn, **kw), *deps)
 
     def quant(name, qc, qs, t, *deps):
         op(name, V, lambda: V.quantize_mx(qc, qs, t), *deps)
@@ -108,61 +111,63 @@ def rank_program(g, core, T, topo):
 
     iota("i.p", T.pidx[:], [[0, 2]], 0, 1, False)
     iota("i.r16", T.r16[:], [[16, 16]], 0, 0, True)
-    iota("i.dup", T.rdup[:], [[16, 16], [0, 2]], 0, 0, True)
-    iota("i.idw0", T.idw0[:], [[1, 384]], 256 * rank - 128, 0, True)
+    iota("i.r32", T.r32[:], [[32, 8], [0, 2]], 0, 0, True)
     op("m.ones", V, lambda: V.memset(T.ones[:], 1.0))
     op("m.zt", V, lambda: V.memset(T.zt[:], 0.0))
     ts("c.and", T.pand[:], T.pidx[:], 15, None, A.bitwise_and, None, "i.p")
-    ts("c.and2", T.pand2[:], T.pidx[:], 16, None, A.bitwise_and, None, "i.p")
+    ts("c.and2", T.pand2[:], T.pidx[:], 31, None, A.bitwise_and, None, "i.p")
     tc("c.pq", T.pq[:], T.pand[:], "c.and")
-    tc("c.hq", T.hq[:], T.pand2[:], "c.and2")
+    tc("c.p31", T.p31[:], T.pand2[:], "c.and2")
     ts("c.jw", T.jw[:], T.r16[:], T.pq[:, 0:1], None, A.add, None, "c.pq", "i.r16")
-    ts("c.hs", T.hs[:], T.hq[:], -0.0625, 16.0, A.mult, A.add, "c.hq")
-
-    def front(b):
-        op("m.d%d" % b, V, lambda t=T["d%d" % b]: V.memset(t[:, 0:16], 256.0))
-
-    def rest(b):
-        ts("c.idx%d" % b, T["idx%d" % b][:, 0:4], T.jw[:, 0:4], -1.0, 255.0, A.mult, A.add, "c.jw")
-        quant("q.z%d" % b, T["z%dc" % b][:, 64:192], T["z%ds" % b][:, 64:192], T.zt[:], "m.zt")
-    front(0)
-    ts("c.offd", T.offd[:], T.rdup[:], T.pq[:, 0:1], T.hs[:, 0:1], A.add, A.add, "c.pq", "c.hs", "i.dup")
-    ts("c.bias", T.bias[:], T.jw[:, 0:2], -255.5, None, A.add, None, "c.jw")
-    ts("c.thr", T.thr[:], T.jw[:, 2:4], -1.0, 256.0, A.mult, A.add, "c.jw")
+    ts("c.offd", T.offd[:], T.r32[:], T.p31[:, 0:1], None, A.add, None, "c.p31", "i.r32")
+    quant("q.z", T.zc[:, 64:192], T.zs[:, 64:192], T.zt[:], "m.zt")
     for b in range(2):
-        scopy("m.h%d" % b, T["h%d" % b][:, 256:512], T.zt[:, 0:256], "m.zt")
+        act("m.h%d" % b, T["h%d" % b][:, 256:512], T.zt[:, 0:256], AF.Copy, "m.zt")
+    for b, w, k in ((0, T.w0, 288), (1, T.w1, 280)):
+        act("m.a%d" % b, w[:, 0:16], T.zt[:, 0:16], AF.Copy, "m.zt")
+        act("m.b%d" % b, w[:, 272:k], T.zt[:, 0:k - 272], AF.Copy, "m.zt")
 
-    for t in range(4):
+    for t in range(3):
         ts("u0.%d" % t, T.ut0[:, t:512:4], T.ones[:, 0:128], T.ub[:, t:t + 1], None, A.mult, None, "ld.u", "m.ones")
-
-    def fill(name, out, col):
-        op(name, S, lambda: S.activation(out, T.zt[:, 0:128], AF.Identity, bias=col), "ld.u", "m.zt")
+    act("u0.3", T.ut0[:, 3:512:4], T.zt[:, 0:128], AF.Identity, "ld.u", "m.zt", bias=T.ub[:, 3:4])
+    act("c.bias", T.bias[:], T.jw[:, 2:4], AF.Copy, "c.jw", scale=128.0, bias=64.0)
+    act("c.lo", T.lo[:], T.jw[:, 0:2], AF.Copy, "c.jw", scale=128.0)
+    act("c.hi", T.hi[:], T.jw[:, 0:2], AF.Copy, "c.jw", scale=128.0, bias=128.0)
+    act("c.ini", T.ini[:], T.jw[:, 0:2], AF.Copy, "c.jw", scale=16384.0, bias=16384.0)
     for t in range(4):
-        fill("u1.%d" % t, T.ut1[:, t:512:4], T.ub[:, 4 + t:5 + t])
+        act("u1.%d" % t, T.ut1[:, t:512:4], T.zt[:, 0:128], AF.Identity, "ld.u", "m.zt", bias=T.ub[:, 4 + t:5 + t])
     quant("q.u0", T.qu0c[:], T.qu0s[:], T.ut0[:], "u0.0", "u0.1", "u0.2", "u0.3")
 
     X = ("q.xA", "q.xB")
     quant("q.xA", T.hold0c[:, 128:256], T.hold0s[:, 128:256], T.xt[:, 0:512], "ld.xA")
-    quant("q.xB", T.hold0c[:, 256:384], T.hold0s[:, 256:384], T.xt[:, 512:1024], "ld.xB")
     mm("t.sA", 0, 128, T.qu0c[:], T.qu0s[:], T.hold0c[:, 128:256], T.hold0s[:, 128:256], "q.u0", "q.xA")
+    act("sg.A", T.siga[:], T.ps0[:, 0:128], AF.Sign, "t.sA", scale=-1.0)
+    act("w.A", T.w0[:, 16:144], T.siga[:], AF.Relu, "sg.A", scale=64.0, accum_out=T.cna[:, 0:1])
+    quant("q.xB", T.hold0c[:, 256:384], T.hold0s[:, 256:384], T.xt[:, 512:1024], "ld.xB")
     mm("t.sB", 1, 128, T.qu0c[:], T.qu0s[:], T.hold0c[:, 256:384], T.hold0s[:, 256:384], "q.u0", "q.xB")
-    ts("w.A", T.w0[:, 0:128], T.ps0[:, 0:128], 0.0, None, A.is_lt, None, "t.sA")
-    scan("d.A", T.d0[:, 16:144], T.ones[:, 0:128], T.w0[:, 0:128], 256.0, A.subtract, "w.A", "m.ones")
-    ts("w.B", T.w0[:, 128:256], T.ps1[:, 0:128], 0.0, None, A.is_lt, None, "t.sB")
-    scan("d.0", T.d0[:, 144:272], T.ones[:, 0:128], T.w0[:, 128:256], T.d0[:, 143:144], A.subtract, "w.B", "d.A")
+    scan("f.A", T.f0[:, 0:128], T.w0[:, 16:144], T.w0[:, 15:143], 0.0, A.add, A.add, "w.A", "m.a0")
+    act("wb.A", T.wb0[:, 0:128], T.w0[:, 15:143], AF.Copy, "w.A", "m.a0", scale=1.015625)
+    ts("w.B", T.w0[:, 144:272], T.ps1[:, 0:128], 0.0, 64.0, A.is_lt, A.mult, "t.sB")
+    scan("f.0", T.f0[:, 128:257], T.w0[:, 144:273], T.w0[:, 143:272], T.f0[:, 127:128], A.add, A.add, "w.B", "f.A", "m.b0")
 
     def lists(b):
-        d, acc, mk, scr, off, junk = (T[k % b] for k in ("d%d", "acc%d", "mk%d", "scr%d", "off%d", "junk%d"))
-        n = "d.%d" % b
+        f, acc, cl, su, off, junk = (T[k % b] for k in ("f%d", "acc%d", "clip%d", "sums%d", "off%d", "junk%d"))
+        n = "f.%d" % b
         for m in range(2):
-            op("ps%d.%d" % (m, b), S, lambda m=m: S.activation(junk[:, 256 * m:256 * m + 255], d[:, 16:271], AF.Sign,
-                                                               bias=T.bias[:, m:m + 1], accum_out=acc[:, m:m + 1]), n, "c.bias")
-        ts("pm2.%d" % b, mk[:, 0:223], d[:, 48:271], T.thr[:, 0:1], None, A.is_ge, None, n, "c.thr")
-        ts("pm3.%d" % b, mk[:, 256:463], d[:, 64:271], T.thr[:, 1:2], None, A.is_ge, None, n)
-        scan("pc2.%d" % b, scr[:, 33:256], T.ones[:, 0:223], mk[:, 0:223], 32.0, A.add, "pm2.%d" % b)
-        scan("pc3.%d" % b, scr[:, 305:512], T.ones[:, 0:207], mk[:, 256:463], 48.0, A.add, "pm3.%d" % b)
-        tc("ov.%d" % b, off[:, 2:4], scr[:, 255:512:256], "pc2.%d" % b, "pc3.%d" % b)
-        ts("os.%d" % b, off[:, 0:2], acc[:, 0:2], 0.5, 127.5, A.mult, A.add, "ps0.%d" % b, "ps1.%d" % b)
+            act("ps%d.%d" % (m, b), junk[:, 128 * m:128 * m + 112], f[:, 33:256:2], AF.Sign, n, "c.bias", scale=-1.0,
+                bias=T.bias[:, m:m + 1], accum_out=acc[:, m:m + 1])
+        for m in range(2):
+            ts("pm%d.%d" % (m, b), cl[:, 128 * m:128 * m + 128], f[:, 1:256:2], T.lo[:, m:m + 1], T.hi[:, m:m + 1], A.max, A.min,
+               n, "c.lo", "c.hi")
+        if not b:
+            ts("n.B", T.cnb[:], f[:, 256:257], T.cna[:, 0:1], T.cna[:, 0:1], A.subtract, A.subtract, n, "w.A")
+        for m in range(2):
+            scan("pc%d.%d" % (m, b), su[:, 128 * m:128 * m + 128], T.ones[:, 0:128], cl[:, 128 * m:128 * m + 128],
+                 T.ini[:, m:m + 1], A.mult, A.subtract, "pm%d.%d" % (m, b), "c.ini")
+        p = 0 if b else 128
+        act("wb.B%d" % b, T["wb%d" % b][:, p:256], T["w%d" % b][:, 15 + p:271], AF.Copy, n, scale=1.015625)
+        ts("os.%d" % b, off[:, 2:4], acc[:, 0:2], 111.0, 144.0, A.min, A.add, "ps0.%d" % b, "ps1.%d" % b)
+        ts("ov.%d" % b, off[:, 0:2], su[:, 127:256:128], 0.015625, 255.0, A.mult, A.min, "pc0.%d" % b, "pc1.%d" % b)
 
     def pick(name, oc, os, ic, is_, off, deps):
         op(name + "c", V, lambda: V.tensor_copy(u32(oc), u32(ic).indirect(off)), *deps)
@@ -173,54 +178,69 @@ def rank_program(g, core, T, topo):
         pick("mg%d%d" % (b, i), oc[:, c + p:c + q], os[:, c + p:c + q], T["hold%dc" % b][:, 0:384], T["hold%ds" % b][:, 0:384],
              T["offm%d" % b][:, 4 + p // 16:4 + q // 16], ("om.%d" % b, "q.n%d" % b) + deps)
 
-    def wrap(b):
-        dp, dq = T["dtr%d" % b][:, 0:512:32], T["dtr%d" % b][:, 16:512:32]
-        scopy("dup.%d" % b, T["dup%d" % b][:], T["d%d" % b][:, 0:272].indirect(T.offd[:, 0:32]), "d.%d" % b, "c.offd", "m.d%d" % b)
+    def escan(b):
+        scan("e.%d" % b, T["e%d" % b][:], T["wb%d" % b][:], T["w%d" % b][:, 16:272], 64.0, A.add, A.subtract, "wb.B%d" % b,
+             "f.%d" % b, *(() if b else ("wb.A",)))
         tc("lf.%d" % b, T["lf%d" % b][:], T["off%d" % b][:, 0:4], "ov.%d" % b, "os.%d" % b)
+        act("dup.%d" % b, T["dup%d" % b][:], T["e%d" % b][:, 0:256].indirect(T.offd[:, 0:16]), AF.Copy, "e.%d" % b, "c.offd")
+
+    def gap4(b):
         tt("g4.%d" % b, T["gap%d" % b][:, 0:4], T["lf%d" % b][:], T.alt[:, 0:4], A.subtract, "lf.%d" % b, "c.alt0")
-        if b == 0:
-            ts("w.1x", T.w1[:, 0:256], T.ps2[:, 0:256], 0.0, None, A.is_lt, None, "t.s1")
+
+    def laid(b):
         op("tr.%d" % b, V, lambda: V.transpose(T["dtr%d" % b][:], T["dup%d" % b][:]), "dup.%d" % b)
-        tt("wl.%d" % b, T["wl%d" % b][:], dp, dq, A.is_lt, "tr.%d" % b)
-        tt("g16.%d" % b, T["gap%d" % b][:, 4:20], T.c16[:], dp, A.subtract, "tr.%d" % b, "c.c16")
-        tt("ix.%d" % b, T["idx%d" % b][:, 4:20], T["wl%d" % b][:], dp, A.mult, "wl.%d" % b)
+
+    def gap16(b):
+        tt("g16.%d" % b, T["gap%d" % b][:, 4:20], T["dtr%d" % b][:, 0:256:16], T.alt[:, 4:20], A.subtract, "tr.%d" % b, "c.alt1")
 
     def settle(b, part):
+        own = T["f%d" % b][:, 256:257]
         if part == 0:
-            ts("th.%d" % b, T.th[:, b:b + 1], T["cnt%d" % b][:, 0:1], T["d%d" % b][:, 271:272], 192.0, A.max, A.max,
-               "A.cnt%d" % b, "d.%d" % b)
-        if part == 1:
-            ts("se.%d" % b, T["sel%d" % b][:], T["idx%d" % b][:], T.th[:, b:b + 1], None, A.is_ge, None,
-               "th.%d" % b, "ix.%d" % b, "c.idx%d" % b)
+            if b:
+                ts("th.1", T.th[:, 1:2], T.cnt1[:, 0:1], own, 8192.0, A.min, A.min, "A.cnt1", "f.1")
+            else:
+                ts("nn.0", T.acnt[:], T.cntb[:, 0:1], T.cnta[:, 0:1], T.cnta[:, 0:1], A.add, A.add, "A.cnta", "A.cntb")
+        if part == 1 and not b:
+            ts("th.0", T.th[:, 0:1], T.acnt[:], own, 8192.0, A.min, A.min, "nn.0", "f.0")
         if part == 2:
-            tt("mv.%d" % b, T["mov%d" % b][:], T["sel%d" % b][:], T["gap%d" % b][:], A.mult, "se.%d" % b, "g4.%d" % b, "g16.%d" % b)
+            ts("s4.%d" % b, T["sel%d" % b][:, 0:4], T.jw[:, 0:4], 128.0, T.th[:, b:b + 1], A.mult, A.is_lt, "th.%d" % b, "c.jw")
+            ts("s16.%d" % b, T["sel%d" % b][:, 4:20], T["dtr%d" % b][:, 0:256:16], 128.0, T.th[:, b:b + 1], A.mult, A.is_lt,
+               "th.%d" % b, "tr.%d" % b)
         if part == 3:
+            tt("mv.%d" % b, T["mov%d" % b][:], T["sel%d" % b][:], T["gap%d" % b][:], A.mult, "s4.%d" % b, "s16.%d" % b,
+               "g4.%d" % b, "g16.%d" % b)
+        if part == 4:
             tt("rs.%d" % b, T["res%d" % b][:], T["mov%d" % b][:], T.alt[:], A.add, "mv.%d" % b, "c.alt0", "c.alt1")
+        if part == 5:
             tc("om.%d" % b, T["offm%d" % b][:], T["res%d" % b][:], "rs.%d" % b)
 
     def expert(b, i):
         a, c = 512 * b + 128 * i, 2048 * b + 512 * i
         quant("q.w%d%d" % (i, b), T.qwc[:, a:a + 128], T.qws[:, a:a + 128], T.wt[:, c:c + 512], "ld.w%d" % b)
 
-    def fresh(b):
-        z, h, hold = "z%d" % b, T["h%d" % b], "hold%d" % b
+    def fresh(b, between=None):
+        h, hold, z = T["h%d" % b], "hold%d" % b, Z[b]
         for i in range(4):
             a = 512 * b + 128 * i
-            mm("R%d.%d" % (i, b), 4 + i, 128, T.qwc[:, a:a + 128], T.qws[:, a:a + 128], T[z + "c"][:, 0:128], T[z + "s"][:, 0:128],
-               "q.w%d%d" % (i, b), "q.z%d" % b, "A.cod%d" % b, "A.scl%d" % b, *(("K%d.0" % i,) if b else ()))
+            mm("R%d.%d" % (i, b), 4 + i, 128, T.qwc[:, a:a + 128], T.qws[:, a:a + 128], T.zc[:, z:z + 128], T.zs[:, z:z + 128],
+               "q.w%d%d" % (i, b), "q.z", "A.cod%d" % b, "A.scl%d" % b, *(("K%d.0" % i,) if b else ()))
         for i in range(4):
+            r = T["ps%d" % (4 + i)][:, NEW[b]:NEW[b] + 64]
             if i == 3:
-                ts("K%d.%d" % (i, b), h[:, i:256:4], T["ps%d" % (4 + i)][:, 0:64], 0.0625, None, A.mult, None, "R%d.%d" % (i, b))
+                ts("K%d.%d" % (i, b), h[:, i:256:4], r, 0.0625, None, A.mult, None, "R%d.%d" % (i, b))
             else:
-                scopy("K%d.%d" % (i, b), h[:, i:256:4], T["ps%d" % (4 + i)][:, 0:64], "R%d.%d" % (i, b), scale=0.0625)
+                act("K%d.%d" % (i, b), h[:, i:256:4], r, AF.Copy, "R%d.%d" % (i, b), scale=0.0625)
+                if i == 0 and between is not None:
+                    between()
         quant("q.n%d" % b, T[hold + "c"][:, 0:128], T[hold + "s"][:, 0:128], h[:],
               *["K%d.%d" % (i, b) for i in range(4)], "m.h%d" % b)
 
-    send("g.cnt0", mate0, T.cnt0[:, 0:1], T.d0[:, 271:272], "rcnt0", "d.0", lsem="lcnt0")
+    send("g.cnta", mate0, T.cnta[:, 0:1], T.cna[:, 0:1], "rcnta", "w.A", lsem="lcnt")
     lists(0)
+    send("g.cntb", mate0, T.cntb[:, 0:1], T.cnb[:, 0:1], "rcntb", "n.B")
     pick("pk0", T.snd0c[:], T.snd0s[:], T.hold0c[:, 128:384], T.hold0s[:, 128:384], T.off0[:, 0:4], ("ov.0", "os.0") + X)
-    send("g.cod0", mate0, u8(T.z0c[:, 0:64]), u8(T.snd0c[:, 0:64]), "rcod0", "pk0c")
-    send("g.scl0", mate0, T.z0s[:, 0:64], T.snd0s[:, 0:64], "rscl0", "pk0s")
+    send("g.cod0", mate0, u8(T.zc[:, 0:64]), u8(T.snd0c[:, 0:64]), "rcod0", "pk0c")
+    send("g.scl0", mate0, T.zs[:, 0:64], T.snd0s[:, 0:64], "rscl0", "pk0s")
     to = [topo.addr(cores[r]) for r in (mate0, far)]
     local["lall"] += eng(rank, mate0)
     op("g.lst", g, lambda: g.remote_dma_fused([RemoteDMATransfer(
@@ -228,74 +248,80 @@ def rank_program(g, core, T, topo):
         dma_engine_mask=topo.mask(core, cores[mate0]) & topo.mask(core, cores[far]),
         remote_sem=T.sem["rlst"], srcs=[T.off0[:, 0:4]], dsts=[T.lin[:], T.lin2[:]])], local_sem=T.sem["lall"]), "ov.0", "os.0")
     op("g.go", g, lambda: g.sem_inc(T.sem["go"], 1))
-    move("ld.v", Y, T.vt[:], T.v[:], "E.go", "L.cnt0")
+    move("ld.v", Y, T.vt[:], T.v[:], "E.go", "L.cnt")
     move("ld.w1", Y, T.wt[:, 2048:4096], T.w[:, 2048:4096])
-    iota("i.tabp", T.tabp[:], [[1, 256]], 256 * mate0, 0, True)
-    iota("i.tabq", T.tabq[:], [[1, 256]], 256 * far, 0, True)
-    iota("i.pid", T.pid[:], [[1, 320]], 256 * mate1, 0, True)
-    iota("i.idw1", T.idw1[:, 64:128], [[1, 64]], 0, 0, True)
+    iota("i.row", T.row[:], [[1, 256]], 0, 0, True)
+    iota("i.idw0", T.idw0[:], [[1, 384]], 256 * rank - 128, 0, True)
 
+    act("c.alt0", T.alt[:, 0:4], T.jw[:, 0:4], AF.Copy, "c.jw", bias=264.0)
+    act("c.alt1", T.alt[:, 4:20], T.jw[:], AF.Copy, "c.jw", bias=128.0)
+    escan(0)
     quant("q.u1", T.qu1c[:], T.qu1s[:], T.ut1[:], "u1.0", "u1.1", "u1.2", "u1.3")
     mm("t.s1", 2, 256, T.qu1c[:], T.qu1s[:], T.hold0c[:, 128:384], T.hold0s[:, 128:384], "q.u1", *X)
-    ts("c.alt0", T.alt[:, 0:4], T.jw[:, 0:4], 256.0, None, A.add, None, "c.jw")
-    ts("c.alt1", T.alt[:, 4:20], T.jw[:], 128.0, None, A.add, None, "c.jw")
-    ts("c.c16", T.c16[:], T.jw[:], -1.0, 127.0, A.mult, A.add, "c.jw")
-    rest(0)
-    wrap(0)
-    for i, part in ((0, None), (1, 0), (2, 1), (3, 2)):
-        expert(0, i)
-        if part is not None:
-            settle(0, part)
-    settle(0, 3)
-    front(1)
-    rest(1)
+    act("sg.1", T.sig[:], T.ps2[:, 0:256], AF.Sign, "t.s1", scale=-1.0)
+    act("w.1x", T.w1[:, 16:272], T.sig[:], AF.Relu, "sg.1", scale=64.0)
+    expert(0, 0)
+    gap4(0)
+    expert(0, 1)
+    expert(0, 2)
+    expert(0, 3)
+    laid(0)
+    settle(0, 0)
+    gap16(0)
+    for part in range(1, 6):
+        settle(0, part)
     send("g.pof", mate1, T.pof[:], T.offm0[:, 0:4], "rpof", "om.0")
+    iota("i.pid", T.pid[:, 0:256], [[1, 256]], 256 * mate1, 0, True)
+    iota("i.idw1", T.idw1[:, 64:128], [[1, 64]], 0, 0, True)
 
     fresh(0)
-    mm("t.sN", 0, 128, T.qu1c[:], T.qu1s[:], T.hold0c[:, 0:128], T.hold0s[:, 0:128], "q.n0", "w.A")
+    mm("t.sN", 0, 128, T.qu1c[:], T.qu1s[:], T.hold0c[:, 0:128], T.hold0s[:, 0:128], "q.n0", "sg.A")
     merge(0, 0, 0, 160, *X)
-    ts("w.N", T.wn[:], T.ps0[:, 0:64], 0.0, None, A.is_lt, None, "t.sN")
+    ts("w.N", T.wn[:], T.ps0[:, 0:64], 0.0, 64.0, A.is_lt, A.mult, "t.sN")
     merge(0, 1, 160, 192, *X)
-    tc("w.1", T.w1[:, 0:320].indirect(T.offm0[:, 0:4]), T.wn[:], "w.N", "w.1x", "om.0")
+    tc("w.1", T.w1[:, 16:352].indirect(T.offm0[:, 0:4]), T.wn[:], "w.N", "w.1x", "om.0")
     merge(0, 2, 192, 224, *X)
-    scan("d.1", T.d1[:, 16:272], T.ones[:], T.w1[:, 0:256], 256.0, A.subtract, "w.1")
+    scan("f.1", T.f1[:, 0:257], T.w1[:, 16:273], T.w1[:, 15:272], 0.0, A.add, A.add, "w.1", "m.a1", "m.b1")
 
-    send("g.cnt1", mate1, T.cnt1[:, 0:1], T.d1[:, 271:272], "rcnt1", "d.1")
+    send("g.cnt1", mate1, T.cnt1[:, 0:1], T.f1[:, 256:257], "rcnt1", "f.1")
     merge(0, 3, 224, 256, *X)
+    act("id.p", T.ptmp[:], T.row[:].indirect(T.lin2[:, 0:4]), AF.Copy, "A.lst", "i.row", bias=float(256 * far))
+    act("id.a", T.idw0[:, 0:64], T.row[:].indirect(T.lin[:, 0:4]), AF.Copy, "A.lst", "i.row", "i.idw0", bias=float(256 * mate0))
     lists(1)
     M = tuple("mg0%d%s" % (i, k) for i in range(4) for k in "cs")
     pick("pk1", T.snd1c[:], T.snd1s[:], T.hold1c[:, 128:384], T.hold1s[:, 128:384], T.off1[:, 0:4], ("ov.1", "os.1") + M)
-    send("g.cod1", mate1, u8(T.z1c[:, 0:64]), u8(T.snd1c[:, 0:64]), "rcod1", "pk1c")
-    send("g.scl1", mate1, T.z1s[:, 0:64], T.snd1s[:, 0:64], "rscl1", "pk1s")
+    send("g.cod1", mate1, u8(T.zc[:, 192:256]), u8(T.snd1c[:, 0:64]), "rcod1", "pk1c")
+    send("g.scl1", mate1, T.zs[:, 192:256], T.snd1s[:, 0:64], "rscl1", "pk1s")
     send("g.lst1", mate1, T.lin1[:], T.off1[:, 0:4], "rlst1", "ov.1", "os.1")
+    escan(1)
     quant("q.v", T.qvc[:], T.qvs[:], T.vt[:], "ld.v")
     mm("t.y", 3, 256, T.qvc[:], T.qvs[:], T.hold1c[:, 128:384], T.hold1s[:, 128:384], "q.v", *M)
+    gap4(1)
     for i in range(4):
         expert(1, i)
+    laid(1)
     settle(1, 0)
-    wrap(1)
-    scopy("id.p", T.ptmp[:], T.tabq[:].indirect(T.lin2[:, 0:4]), "A.lst", "i.tabq")
-    scopy("id.a", T.idw0[:, 0:64], T.tabp[:].indirect(T.lin[:, 0:4]), "A.lst", "i.tabp", "i.idw0")
-    tc("id.q", T.pid[:, 0:320].indirect(T.pof[:, 0:4]), T.ptmp[:], "A.pof", "id.p", "i.pid")
-    for part in (1, 2, 3):
+    gap16(1)
+    settle(1, 2)
+    tc("id.q", T.pid[:, 0:336].indirect(T.pof[:, 0:4]), T.ptmp[:], "A.pof", "id.p", "i.pid")
+    for part in range(3, 6):
         settle(1, part)
-    ts("ks", T.ksb[:], T.th[:], -1.0, 256.0, A.mult, A.add, "th.0", "th.1")
-    scopy("id.m", T.idw1[:, 128:384], T.idw0[:].indirect(T.offm0[:, 4:20]), "id.a", "i.idw0", "om.0")
-    scopy("y.m", T.yrow[:, 0:256], T.ps3[:, 0:256], "t.y")
-    fresh(1)
-    scopy("id.n", T.idw1[:, 0:64], T.pid[:, 0:256].indirect(T.lin1[:, 0:4]), "id.q", "A.lst1")
-    scopy("id.f", T.idf[:], T.idw1[:].indirect(T.offm1[:, 4:20]), "id.m", "id.n", "i.idw1", "om.1")
+    ts("ks", T.ksb[:], T.th[:], 0.0078125, None, A.mult, None, "th.0", "th.1")
+    act("id.m", T.idw1[:, 128:384], T.idw0[:].indirect(T.offm0[:, 4:20]), AF.Copy, "id.a", "i.idw0", "om.0")
+    act("y.m", T.yrow[:, 0:256], T.ps3[:, 0:256], AF.Copy, "t.y")
+    fresh(1, lambda: act("id.n", T.idw1[:, 0:64], T.pid[:, 0:256].indirect(T.lin1[:, 0:4]), AF.Copy, "id.q", "A.lst1"))
+    act("id.f", T.idf[:], T.idw1[:].indirect(T.offm1[:, 4:20]), AF.Copy, "id.m", "id.n", "i.idw1", "om.1")
     mm("t.yn", 1, 128, T.qvc[:], T.qvs[:], T.hold1c[:, 0:128], T.hold1s[:, 0:128], "q.n1", "q.v", "w.B")
-    scopy("y.n", T.yn[:], T.ps1[:, 0:64], "t.yn")
+    act("y.n", T.yn[:], T.ps1[:, 0:64], AF.Copy, "t.yn")
     merge(1, 0, 0, 256, *M)
-    tc("y.s", T.yrow[:, 0:320].indirect(T.offm1[:, 0:4]), T.yn[:], "y.n", "y.m", "om.1")
+    tc("y.s", T.yrow[:, 0:336].indirect(T.offm1[:, 0:4]), T.yn[:], "y.n", "y.m", "om.1")
 
     move("st.k", Y, T.ks[0:1, 0:2], T.ksb[0:1, 0:2], "ks")
+    move("st.i", Y, T.ids[0:1, :], T.idf[0:1, :], "id.f")
     move("st.c", Y, T.oc[:, :], u8(T.finc[:, 0:256]), "mg10c")
     move("st.y", Y, T.y[:, :], T.yrow[:, 0:256], "y.s")
     for k in range(4):
-        move("st.s%d" % k, S if k < 2 else Y, T.osc[4 * k:4 * k + 4, 0:256], T.fins[32 * k:32 * k + 4, 0:256], "mg10s")
-    move("st.i", S, T.ids[0:1, :], T.idf[0:1, :], "id.f")
+        move("st.s%d" % k, S if k < 3 else Y, T.osc[4 * k:4 * k + 4, 0:256], T.fins[32 * k:32 * k + 4, 0:256], "mg10s")
     op("end", Y, None, "st.k", "st.i", "st.c", "st.y", "st.s0", "st.s1", "st.s2", "st.s3")
 
     qs = (g, V, S, P, Y)

from concourse.bass import DstId, RemoteDMATransfer
from concourse.mybir import dt, AluOpType as A, ActivationFunctionType as AF

F8, BF = "float8_e4m3fn_x4", "bfloat16"


def _sb(n, t="float32"):
    return ("sbuf", [128, n], t)


SCRATCH = {
    "cna": _sb(1), "cnb": _sb(1, BF), "cnta": _sb(1), "cntb": _sb(1, BF), "cnt1": _sb(1, BF),
    "lin": _sb(4, "uint16"), "lin2": _sb(4, "uint16"), "pof": _sb(4, "uint16"),
    "lin1": _sb(4, "uint16"), "offd": _sb(16, "uint16"), "pidx": _sb(2, "int32"), "pand": _sb(2, "int32"), "pand2": _sb(2, "int32"),
}
for _n, _k in dict(ub=8, xt=1024, wt=4096, vt=512, ut0=512, ut1=512, zt=512, ones=128, h0=512, h1=512, w0=288, w1=352, wn=64,
                   sig=256, siga=128).items():
    SCRATCH[_n] = _sb(_k, BF)
for _n, _k in dict(qu0=128, qu1=128, qw=1024, qv=128, hold0=384, hold1=384, fin=256, snd0=64, snd1=64, z=256).items():
    SCRATCH[_n + "c"], SCRATCH[_n + "s"] = _sb(_k, F8), _sb(_k, "uint8")
for _n, _k in dict(pq=2, p31=2, r16=16, r32=16, jw=16, bias=2, lo=2, hi=2, ini=2, alt=20, acnt=1, th=2, ksb=2, row=256, pid=336,
                   ptmp=64, idw0=384, idw1=384, idf=256, yrow=336, yn=64).items():
    SCRATCH[_n] = _sb(_k)
for _b in "01":
    for _n, _k in dict(f=272, junk=256, clip=256, sums=256, wb=256, e=256, dup=256, dtr=256).items():
        SCRATCH[_n + _b] = _sb(_k, BF)
    for _n, _k in dict(acc=2, lf=4, gap=20, sel=20, mov=20, res=20).items():
        SCRATCH[_n + _b] = _sb(_k)
    SCRATCH["off" + _b], SCRATCH["offm" + _b] = _sb(4, "uint16"), _sb(20, "uint16")
for _b in range(8):
    SCRATCH["ps%d" % _b] = ("psum", [128, 512], "float32")

REMOTE = ["rcnta", "rcntb", "rcod0", "rscl0", "rlst", "rpof", "rcnt1", "rlst1", "rcod1", "rscl1", "lall", "lcnt", "go"]
POOL = 80
SEMAPHORES = REMOTE + ["s%d" % _i for _i in range(POOL)]
Z = (0, 128)
NEW = (0, 64)


def rank_program(g, core, T, topo):
    rank = T.rank_of(core)
    if rank is None:
        return
    cores = T.cores
    mate0, mate1, far = rank ^ 1, rank ^ 2, rank ^ 3
    V, S, P, Y = g.vector, g.scalar, g.tensor, g.sync
    ops, local = [], {"lall": 0, "lcnt": 0}

    def op(name, queue, fn, *deps, dma=False):
        ops.append((name, queue, fn, deps, dma))

    def eng(a, b):
        return len(topo.engines(cores[a], cores[b]))
    arrive = {"A.lst": ("rlst", eng(mate0, rank) + eng(far, rank)), "A.pof": ("rpof", eng(mate1, rank)),
              "A.lst1": ("rlst1", eng(mate1, rank)), "A.cnt1": ("rcnt1", eng(mate1, rank)),
              "A.cnta": ("rcnta", eng(mate0, rank)), "A.cntb": ("rcntb", eng(mate0, rank)),
              "E.go": ("go", 1), "L.cnt": ("lcnt", eng(rank, mate0))}
    for b, m in ((0, mate0), (1, mate1)):
        for kind in ("cod", "scl"):
            arrive["A.%s%d" % (kind, b)] = ("r%s%d" % (kind, b), eng(m, rank))

    def send(name, to, dst, src, sem, *deps, lsem="lall"):
        rid, pid, _ = topo.addr(cores[to])
        local[lsem] += eng(rank, to)
        op(name, g, lambda: g.remote_dma(out_ap=dst, in_ap=src, remote_sem=T.sem[sem], local_sem=T.sem[lsem], pid=pid,
                                         routing_id=rid, dma_engine_mask=topo.mask(core, cores[to])), *deps)

    def u8(v):
        return v.bitcast(dt.uint8)

    def u32(v):
        return v.bitcast(dt.uint32)

    def mm(name, bank, n, wc, ws, xc, xs, *deps):
        op(name, P, lambda: P.matmul_mx(T["ps%d" % bank][:, 0:n], wc, ws, xc, xs, True, True), *deps)

    def ts(name, out, in0, s1, s2, o0, o1, *deps):
        if o1 is None:
            op(name, V, lambda: V.tensor_scalar(out, in0, s1, None, o0), *deps)
        else:
            op(name, V, lambda: V.tensor_scalar(out, in0, s1, s2, o0, o1), *deps)

    def tt(name, out, a, b, o, *deps):
        op(name, V, lambda: V.tensor_tensor(out, a, b, o), *deps)

    def tc(name, out, in_, *deps):
        op(name, V, lambda: V.tensor_copy(out, in_), *deps)

    def scan(name, out, a, b, init, o0, o1, *deps):
        op(name, V, lambda: V.tensor_tensor_scan(out, a, b, init, o0, o1), *deps)

    def act(name, out, in_, fn, *deps, **kw):
        op(name, S, lambda: S.activation(out, in_, fn, **kw), *deps)

    def quant(name, qc, qs, t, *deps):
        op(name, V, lambda: V.quantize_mx(qc, qs, t), *deps)

    def move(name, q, out, in_, *deps):
        op(name, q, lambda: q.dma_start(out, in_), *deps, dma=True)

    def iota(name, out, pattern, base, cm, flag):
        if flag:
            op(name, g, lambda: g.iota(out, pattern, base, cm, allow_small_or_imprecise_dtypes=True))
        else:
            op(name, g, lambda: g.iota(out, pattern, base, cm))

    move("ld.u", S, T.ub[:, 0:8], T.u[:, 0:8])
    move("ld.xA", Y, T.xt[:, 0:512], T.x[:, 0:512])
    move("ld.xB", Y, T.xt[:, 512:1024], T.x[:, 512:1024])
    move("ld.w0", Y, T.wt[:, 0:2048], T.w[:, 0:2048])

    iota("i.p", T.pidx[:], [[0, 2]], 0, 1, False)
    iota("i.r16", T.r16[:], [[16, 16]], 0, 0, True)
    iota("i.r32", T.r32[:], [[32, 8], [0, 2]], 0, 0, True)
    op("m.ones", V, lambda: V.memset(T.ones[:], 1.0))
    op("m.zt", V, lambda: V.memset(T.zt[:], 0.0))
    ts("c.and", T.pand[:], T.pidx[:], 15, None, A.bitwise_and, None, "i.p")
    ts("c.and2", T.pand2[:], T.pidx[:], 31, None, A.bitwise_and, None, "i.p")
    tc("c.pq", T.pq[:], T.pand[:], "c.and")
    tc("c.p31", T.p31[:], T.pand2[:], "c.and2")
    ts("c.jw", T.jw[:], T.r16[:], T.pq[:, 0:1], None, A.add, None, "c.pq", "i.r16")
    ts("c.offd", T.offd[:], T.r32[:], T.p31[:, 0:1], None, A.add, None, "c.p31", "i.r32")
    quant("q.z", T.zc[:, 64:192], T.zs[:, 64:192], T.zt[:], "m.zt")
    for b in range(2):
        act("m.h%d" % b, T["h%d" % b][:, 256:512], T.zt[:, 0:256], AF.Copy, "m.zt")
    for b, w, k in ((0, T.w0, 288), (1, T.w1, 280)):
        act("m.a%d" % b, w[:, 0:16], T.zt[:, 0:16], AF.Copy, "m.zt")
        act("m.b%d" % b, w[:, 272:k], T.zt[:, 0:k - 272], AF.Copy, "m.zt")

    for t in range(3):
        ts("u0.%d" % t, T.ut0[:, t:512:4], T.ones[:, 0:128], T.ub[:, t:t + 1], None, A.mult, None, "ld.u", "m.ones")
    act("u0.3", T.ut0[:, 3:512:4], T.zt[:, 0:128], AF.Identity, "ld.u", "m.zt", bias=T.ub[:, 3:4])
    act("c.bias", T.bias[:], T.jw[:, 2:4], AF.Copy, "c.jw", scale=128.0, bias=64.0)
    act("c.lo", T.lo[:], T.jw[:, 0:2], AF.Copy, "c.jw", scale=128.0)
    act("c.hi", T.hi[:], T.jw[:, 0:2], AF.Copy, "c.jw", scale=128.0, bias=128.0)
    act("c.ini", T.ini[:], T.jw[:, 0:2], AF.Copy, "c.jw", scale=16384.0, bias=16384.0)
    for t in range(4):
        act("u1.%d" % t, T.ut1[:, t:512:4], T.zt[:, 0:128], AF.Identity, "ld.u", "m.zt", bias=T.ub[:, 4 + t:5 + t])
    quant("q.u0", T.qu0c[:], T.qu0s[:], T.ut0[:], "u0.0", "u0.1", "u0.2", "u0.3")

    X = ("q.xA", "q.xB")
    quant("q.xA", T.hold0c[:, 128:256], T.hold0s[:, 128:256], T.xt[:, 0:512], "ld.xA")
    mm("t.sA", 0, 128, T.qu0c[:], T.qu0s[:], T.hold0c[:, 128:256], T.hold0s[:, 128:256], "q.u0", "q.xA")
    act("sg.A", T.siga[:], T.ps0[:, 0:128], AF.Sign, "t.sA", scale=-1.0)
    act("w.A", T.w0[:, 16:144], T.siga[:], AF.Relu, "sg.A", scale=64.0, accum_out=T.cna[:, 0:1])
    quant("q.xB", T.hold0c[:, 256:384], T.hold0s[:, 256:384], T.xt[:, 512:1024], "ld.xB")
    mm("t.sB", 1, 128, T.qu0c[:], T.qu0s[:], T.hold0c[:, 256:384], T.hold0s[:, 256:384], "q.u0", "q.xB")
    scan("f.A", T.f0[:, 0:128], T.w0[:, 16:144], T.w0[:, 15:143], 0.0, A.add, A.add, "w.A", "m.a0")
    act("wb.A", T.wb0[:, 0:128], T.w0[:, 15:143], AF.Copy, "w.A", "m.a0", scale=1.015625)
    ts("w.B", T.w0[:, 144:272], T.ps1[:, 0:128], 0.0, 64.0, A.is_lt, A.mult, "t.sB")
    scan("f.0", T.f0[:, 128:257], T.w0[:, 144:273], T.w0[:, 143:272], T.f0[:, 127:128], A.add, A.add, "w.B", "f.A", "m.b0")

    def lists(b):
        f, acc, cl, su, off, junk = (T[k % b] for k in ("f%d", "acc%d", "clip%d", "sums%d", "off%d", "junk%d"))
        n = "f.%d" % b
        for m in range(2):
            act("ps%d.%d" % (m, b), junk[:, 128 * m:128 * m + 112], f[:, 33:256:2], AF.Sign, n, "c.bias", scale=-1.0,
                bias=T.bias[:, m:m + 1], accum_out=acc[:, m:m + 1])
        for m in range(2):
            ts("pm%d.%d" % (m, b), cl[:, 128 * m:128 * m + 128], f[:, 1:256:2], T.lo[:, m:m + 1], T.hi[:, m:m + 1], A.max, A.min,
               n, "c.lo", "c.hi")
        if not b:
            ts("n.B", T.cnb[:], f[:, 256:257], T.cna[:, 0:1], T.cna[:, 0:1], A.subtract, A.subtract, n, "w.A")
        for m in range(2):
            scan("pc%d.%d" % (m, b), su[:, 128 * m:128 * m + 128], T.ones[:, 0:128], cl[:, 128 * m:128 * m + 128],
                 T.ini[:, m:m + 1], A.mult, A.subtract, "pm%d.%d" % (m, b), "c.ini")
        p = 0 if b else 128
        act("wb.B%d" % b, T["wb%d" % b][:, p:256], T["w%d" % b][:, 15 + p:271], AF.Copy, n, scale=1.015625)
        ts("os.%d" % b, off[:, 2:4], acc[:, 0:2], 111.0, 144.0, A.min, A.add, "ps0.%d" % b, "ps1.%d" % b)
        ts("ov.%d" % b, off[:, 0:2], su[:, 127:256:128], 0.015625, 255.0, A.mult, A.min, "pc0.%d" % b, "pc1.%d" % b)

    def pick(name, oc, os, ic, is_, off, deps):
        op(name + "c", V, lambda: V.tensor_copy(u32(oc), u32(ic).indirect(off)), *deps)
        op(name + "s", S, lambda: S.activation(os, is_.indirect(off), AF.Copy), *deps)

    def merge(b, i, p, q, *deps):
        oc, os, c = (T.finc, T.fins, 0) if b else (T.hold1c, T.hold1s, 128)
        pick("mg%d%d" % (b, i), oc[:, c + p:c + q], os[:, c + p:c + q], T["hold%dc" % b][:, 0:384], T["hold%ds" % b][:, 0:384],
             T["offm%d" % b][:, 4 + p // 16:4 + q // 16], ("om.%d" % b, "q.n%d" % b) + deps)

    def escan(b):
        scan("e.%d" % b, T["e%d" % b][:], T["wb%d" % b][:], T["w%d" % b][:, 16:272], 64.0, A.add, A.subtract, "wb.B%d" % b,
             "f.%d" % b, *(() if b else ("wb.A",)))
        tc("lf.%d" % b, T["lf%d" % b][:], T["off%d" % b][:, 0:4], "ov.%d" % b, "os.%d" % b)
        act("dup.%d" % b, T["dup%d" % b][:], T["e%d" % b][:, 0:256].indirect(T.offd[:, 0:16]), AF.Copy, "e.%d" % b, "c.offd")

    def gap4(b):
        tt("g4.%d" % b, T["gap%d" % b][:, 0:4], T["lf%d" % b][:], T.alt[:, 0:4], A.subtract, "lf.%d" % b, "c.alt0")

    def laid(b):
        op("tr.%d" % b, V, lambda: V.transpose(T["dtr%d" % b][:], T["dup%d" % b][:]), "dup.%d" % b)

    def gap16(b):
        tt("g16.%d" % b, T["gap%d" % b][:, 4:20], T["dtr%d" % b][:, 0:256:16], T.alt[:, 4:20], A.subtract, "tr.%d" % b, "c.alt1")

    def settle(b, part):
        own = T["f%d" % b][:, 256:257]
        if part == 0:
            if b:
                ts("th.1", T.th[:, 1:2], T.cnt1[:, 0:1], own, 8192.0, A.min, A.min, "A.cnt1", "f.1")
            else:
                ts("nn.0", T.acnt[:], T.cntb[:, 0:1], T.cnta[:, 0:1], T.cnta[:, 0:1], A.add, A.add, "A.cnta", "A.cntb")
        if part == 1 and not b:
            ts("th.0", T.th[:, 0:1], T.acnt[:], own, 8192.0, A.min, A.min, "nn.0", "f.0")
        if part == 2:
            ts("s4.%d" % b, T["sel%d" % b][:, 0:4], T.jw[:, 0:4], 128.0, T.th[:, b:b + 1], A.mult, A.is_lt, "th.%d" % b, "c.jw")
            ts("s16.%d" % b, T["sel%d" % b][:, 4:20], T["dtr%d" % b][:, 0:256:16], 128.0, T.th[:, b:b + 1], A.mult, A.is_lt,
               "th.%d" % b, "tr.%d" % b)
        if part == 3:
            tt("mv.%d" % b, T["mov%d" % b][:], T["sel%d" % b][:], T["gap%d" % b][:], A.mult, "s4.%d" % b, "s16.%d" % b,
               "g4.%d" % b, "g16.%d" % b)
        if part == 4:
            tt("rs.%d" % b, T["res%d" % b][:], T["mov%d" % b][:], T.alt[:], A.add, "mv.%d" % b, "c.alt0", "c.alt1")
        if part == 5:
            tc("om.%d" % b, T["offm%d" % b][:], T["res%d" % b][:], "rs.%d" % b)

    def expert(b, i):
        a, c = 512 * b + 128 * i, 2048 * b + 512 * i
        quant("q.w%d%d" % (i, b), T.qwc[:, a:a + 128], T.qws[:, a:a + 128], T.wt[:, c:c + 512], "ld.w%d" % b)

    def fresh(b, between=None):
        h, hold, z = T["h%d" % b], "hold%d" % b, Z[b]
        for i in range(4):
            a = 512 * b + 128 * i
            mm("R%d.%d" % (i, b), 4 + i, 128, T.qwc[:, a:a + 128], T.qws[:, a:a + 128], T.zc[:, z:z + 128], T.zs[:, z:z + 128],
               "q.w%d%d" % (i, b), "q.z", "A.cod%d" % b, "A.scl%d" % b, *(("K%d.0" % i,) if b else ()))
        for i in range(4):
            r = T["ps%d" % (4 + i)][:, NEW[b]:NEW[b] + 64]
            if i == 3:
                ts("K%d.%d" % (i, b), h[:, i:256:4], r, 0.0625, None, A.mult, None, "R%d.%d" % (i, b))
            else:
                act("K%d.%d" % (i, b), h[:, i:256:4], r, AF.Copy, "R%d.%d" % (i, b), scale=0.0625)
                if i == 0 and between is not None:
                    between()
        quant("q.n%d" % b, T[hold + "c"][:, 0:128], T[hold + "s"][:, 0:128], h[:],
              *["K%d.%d" % (i, b) for i in range(4)], "m.h%d" % b)

    send("g.cnta", mate0, T.cnta[:, 0:1], T.cna[:, 0:1], "rcnta", "w.A", lsem="lcnt")
    lists(0)
    send("g.cntb", mate0, T.cntb[:, 0:1], T.cnb[:, 0:1], "rcntb", "n.B")
    pick("pk0", T.snd0c[:], T.snd0s[:], T.hold0c[:, 128:384], T.hold0s[:, 128:384], T.off0[:, 0:4], ("ov.0", "os.0") + X)
    send("g.cod0", mate0, u8(T.zc[:, 0:64]), u8(T.snd0c[:, 0:64]), "rcod0", "pk0c")
    send("g.scl0", mate0, T.zs[:, 0:64], T.snd0s[:, 0:64], "rscl0", "pk0s")
    to = [topo.addr(cores[r]) for r in (mate0, far)]
    local["lall"] += eng(rank, mate0)
    op("g.lst", g, lambda: g.remote_dma_fused([RemoteDMATransfer(
        dst_ids=[DstId(rid=a[0], pnc=a[1]) for a in to],
        dma_engine_mask=topo.mask(core, cores[mate0]) & topo.mask(core, cores[far]),
        remote_sem=T.sem["rlst"], srcs=[T.off0[:, 0:4]], dsts=[T.lin[:], T.lin2[:]])], local_sem=T.sem["lall"]), "ov.0", "os.0")
    op("g.go", g, lambda: g.sem_inc(T.sem["go"], 1))
    move("ld.v", Y, T.vt[:], T.v[:], "E.go", "L.cnt")
    move("ld.w1", Y, T.wt[:, 2048:4096], T.w[:, 2048:4096])
    iota("i.row", T.row[:], [[1, 256]], 0, 0, True)
    iota("i.idw0", T.idw0[:], [[1, 384]], 256 * rank - 128, 0, True)

    act("c.alt0", T.alt[:, 0:4], T.jw[:, 0:4], AF.Copy, "c.jw", bias=264.0)
    act("c.alt1", T.alt[:, 4:20], T.jw[:], AF.Copy, "c.jw", bias=128.0)
    escan(0)
    quant("q.u1", T.qu1c[:], T.qu1s[:], T.ut1[:], "u1.0", "u1.1", "u1.2", "u1.3")
    mm("t.s1", 2, 256, T.qu1c[:], T.qu1s[:], T.hold0c[:, 128:384], T.hold0s[:, 128:384], "q.u1", *X)
    act("sg.1", T.sig[:], T.ps2[:, 0:256], AF.Sign, "t.s1", scale=-1.0)
    act("w.1x", T.w1[:, 16:272], T.sig[:], AF.Relu, "sg.1", scale=64.0)
    expert(0, 0)
    gap4(0)
    expert(0, 1)
    expert(0, 2)
    expert(0, 3)
    laid(0)
    settle(0, 0)
    gap16(0)
    for part in range(1, 6):
        settle(0, part)
    send("g.pof", mate1, T.pof[:], T.offm0[:, 0:4], "rpof", "om.0")
    iota("i.pid", T.pid[:, 0:256], [[1, 256]], 256 * mate1, 0, True)
    iota("i.idw1", T.idw1[:, 64:128], [[1, 64]], 0, 0, True)

    fresh(0)
    mm("t.sN", 0, 128, T.qu1c[:], T.qu1s[:], T.hold0c[:, 0:128], T.hold0s[:, 0:128], "q.n0", "sg.A")
    merge(0, 0, 0, 160, *X)
    ts("w.N", T.wn[:], T.ps0[:, 0:64], 0.0, 64.0, A.is_lt, A.mult, "t.sN")
    merge(0, 1, 160, 192, *X)
    tc("w.1", T.w1[:, 16:352].indirect(T.offm0[:, 0:4]), T.wn[:], "w.N", "w.1x", "om.0")
    merge(0, 2, 192, 224, *X)
    scan("f.1", T.f1[:, 0:257], T.w1[:, 16:273], T.w1[:, 15:272], 0.0, A.add, A.add, "w.1", "m.a1", "m.b1")

    send("g.cnt1", mate1, T.cnt1[:, 0:1], T.f1[:, 256:257], "rcnt1", "f.1")
    merge(0, 3, 224, 256, *X)
    act("id.p", T.ptmp[:], T.row[:].indirect(T.lin2[:, 0:4]), AF.Copy, "A.lst", "i.row", bias=float(256 * far))
    act("id.a", T.idw0[:, 0:64], T.row[:].indirect(T.lin[:, 0:4]), AF.Copy, "A.lst", "i.row", "i.idw0", bias=float(256 * mate0))
    lists(1)
    M = tuple("mg0%d%s" % (i, k) for i in range(4) for k in "cs")
    pick("pk1", T.snd1c[:], T.snd1s[:], T.hold1c[:, 128:384], T.hold1s[:, 128:384], T.off1[:, 0:4], ("ov.1", "os.1") + M)
    send("g.cod1", mate1, u8(T.zc[:, 192:256]), u8(T.snd1c[:, 0:64]), "rcod1", "pk1c")
    send("g.scl1", mate1, T.zs[:, 192:256], T.snd1s[:, 0:64], "rscl1", "pk1s")
    send("g.lst1", mate1, T.lin1[:], T.off1[:, 0:4], "rlst1", "ov.1", "os.1")
    escan(1)
    quant("q.v", T.qvc[:], T.qvs[:], T.vt[:], "ld.v")
    mm("t.y", 3, 256, T.qvc[:], T.qvs[:], T.hold1c[:, 128:384], T.hold1s[:, 128:384], "q.v", *M)
    gap4(1)
    for i in range(4):
        expert(1, i)
    laid(1)
    settle(1, 0)
    gap16(1)
    settle(1, 2)
    tc("id.q", T.pid[:, 0:336].indirect(T.pof[:, 0:4]), T.ptmp[:], "A.pof", "id.p", "i.pid")
    for part in range(3, 6):
        settle(1, part)
    ts("ks", T.ksb[:], T.th[:], 0.0078125, None, A.mult, None, "th.0", "th.1")
    act("id.m", T.idw1[:, 128:384], T.idw0[:].indirect(T.offm0[:, 4:20]), AF.Copy, "id.a", "i.idw0", "om.0")
    act("y.m", T.yrow[:, 0:256], T.ps3[:, 0:256], AF.Copy, "t.y")
    fresh(1, lambda: act("id.n", T.idw1[:, 0:64], T.pid[:, 0:256].indirect(T.lin1[:, 0:4]), AF.Copy, "id.q", "A.lst1"))
    act("id.f", T.idf[:], T.idw1[:].indirect(T.offm1[:, 4:20]), AF.Copy, "id.m", "id.n", "i.idw1", "om.1")
    mm("t.yn", 1, 128, T.qvc[:], T.qvs[:], T.hold1c[:, 0:128], T.hold1s[:, 0:128], "q.n1", "q.v", "w.B")
    act("y.n", T.yn[:], T.ps1[:, 0:64], AF.Copy, "t.yn")
    merge(1, 0, 0, 256, *M)
    tc("y.s", T.yrow[:, 0:336].indirect(T.offm1[:, 0:4]), T.yn[:], "y.n", "y.m", "om.1")

    move("st.k", Y, T.ks[0:1, 0:2], T.ksb[0:1, 0:2], "ks")
    move("st.i", Y, T.ids[0:1, :], T.idf[0:1, :], "id.f")
    move("st.c", Y, T.oc[:, :], u8(T.finc[:, 0:256]), "mg10c")
    move("st.y", Y, T.y[:, :], T.yrow[:, 0:256], "y.s")
    for k in range(4):
        move("st.s%d" % k, S if k < 3 else Y, T.osc[4 * k:4 * k + 4, 0:256], T.fins[32 * k:32 * k + 4, 0:256], "mg10s")
    op("end", Y, None, "st.k", "st.i", "st.c", "st.y", "st.s0", "st.s1", "st.s2", "st.s3")

    qs = (g, V, S, P, Y)
    known, seen, waits, needed = [set() for _ in qs], {}, [], set()

    def number(q):
        return [i for i in range(5) if qs[i] is q][0]
    for name, q, fn, deps, dma in ops:
        i, w = number(q), []
        for dep in deps:
            if dep not in known[i]:
                w.append(dep)
                known[i] |= {dep} | seen.get(dep, set())
                needed.add(dep)
        seen[name] = set(known[i])
        waits.append(w)
    pool, mark = [], {e: arrive[e] for e in arrive}
    for name, q, fn, deps, dma in ops:
        if name in needed:
            i = number(q)
            old = [s for s in pool if not dma and s[0] == i and s[2] in seen[name]]
            if old:
                old[0][2], old[0][3] = name, old[0][3] + 1
                mark[name] = (old[0][1], old[0][3])
            else:
                pool.append([-1 if dma else i, "s%d" % len(pool), name, 16 if dma else 1])
                mark[name] = (pool[-1][1], pool[-1][3])
    for (name, q, fn, deps, dma), w in zip(ops, waits):
        for dep in w:
            q.wait_ge(T.sem[mark[dep][0]], mark[dep][1])
        if fn is not None:
            ins = fn()
            if name in needed:
                ins.then_inc(T.sem[mark[name][0]], 16 if dma else 1)
    g.wait_ge(T.sem["lall"], local["lall"])
